import numpy as np
import ml_dtypes


def mxq(x, axis, fmt="e4m3"):
    dtype, down = {"e4m3": (ml_dtypes.float8_e4m3fn, 7), "e5m2": (ml_dtypes.float8_e5m2, 14)}[fmt]
    v = np.moveaxis(np.asarray(x, np.float32).astype(ml_dtypes.bfloat16).astype(np.float64), axis, -1)
    blocks = v.reshape(v.shape[:-1] + (-1, 32))
    amax = np.abs(blocks).max(-1, keepdims=True)
    byte = np.maximum(np.where(amax > 0, np.frexp(amax)[1] - 1 + 127, 0) - down, 1)
    scale = np.exp2(byte - 127.0)
    codes = (blocks / scale).astype(np.float32).astype(dtype).astype(np.float64)
    return np.moveaxis((codes * scale).reshape(v.shape), -1, axis)


WIDE = False


def mx_kscale(k):
    if not WIDE:
        return np.ones(k)
    levels = np.array([10, -10, 5, -5, 0])
    if k % 512:
        return np.exp2(np.random.permutation(np.resize(levels, k // 32))).repeat(32)
    a = np.empty((k // 512, 16))
    for p in range(k // 512):
        a[p, :8] = np.random.permutation(np.resize(levels, 8))
        for g in range(8):
            far = levels[np.abs(levels - a[p, g]) >= 10]
            a[p, g + 8] = far[np.random.randint(len(far))]
    return np.exp2(a.ravel()).repeat(32)


BF16 = ml_dtypes.bfloat16


def bf(x):
    return np.asarray(x, np.float32).astype(BF16)


def f64(x):
    return np.asarray(x).astype(np.float64)


E2M1 = np.array([0.0, 0.5, 1.0, 1.5, 2.0, 3.0, 4.0, 6.0, -0.0, -0.5, -1.0, -1.5, -2.0, -3.0, -4.0, -6.0])


def pack_weight(w, fmt):
    k, n = w.shape
    w = f64(bf(w)).reshape(k // 32, 32, n)
    amax = np.abs(w).max(1)
    if fmt == "e4m3":
        byte = np.frexp(amax)[1] - 1 + 127 - 7
    else:
        mant, ex = np.frexp(amax / 6.0)
        byte = np.where(mant > 0.5, ex, ex - 1) + 127
    byte = np.clip(np.where(amax > 0, byte, 1), 1, 254)
    scaled = (w * np.exp2(127.0 - byte)[:, None, :]).reshape(k, n).astype(np.float32)
    by_word = np.ascontiguousarray(scaled.reshape(k // 512, 128, 4, n).transpose(0, 1, 3, 2))
    if fmt == "e4m3":
        words = by_word.astype(ml_dtypes.float8_e4m3fn).view(np.uint8)
    else:
        c = by_word.astype(ml_dtypes.float4_e2m1fn).view(np.uint8) & 0xF
        words = c[..., 0::2] | (c[..., 1::2] << 4)
    return np.ascontiguousarray(words), np.ascontiguousarray(byte.astype(np.uint8).reshape(k // 512, 16, n))


def unpack_weight(words, scales, fmt):
    g, p, n, _ = words.shape
    if fmt == "e4m3":
        vals = np.ascontiguousarray(words).view(ml_dtypes.float8_e4m3fn).astype(np.float64)
    else:
        nib = np.empty((g, p, n, 4), np.uint8)
        nib[..., 0::2] = words & 0xF
        nib[..., 1::2] = words >> 4
        vals = E2M1[nib]
    vals = vals * np.repeat(np.exp2(scales.astype(np.float64) - 127.0), 8, axis=1)[..., None]
    return vals.transpose(0, 1, 3, 2).reshape(g * 512, n)
def pack4(w):
    words, scales = pack_weight(w, "e2m1")
    return words.reshape(words.shape[0], 128, -1), scales


def unpack4(words, scales):
    return unpack_weight(words.reshape(words.shape[0], 128, -1, 2), scales, "e2m1")


N, D, H = 1024, 1024, 1024


def draw0():
    s, u = mx_kscale(H), mx_kscale(N)
    inputs = {"g": bf(np.random.standard_normal((N, H)) * (64.0 / np.sqrt(N)) * s[None, :] / (u * u)[:, None]),
              "z": bf(np.random.uniform(0.1, 0.9, (N, H))),
              "c": bf(np.random.uniform(-0.9, 0.9, (N, H))),
              "r": bf(np.random.uniform(0.1, 0.9, (N, H))),
              "h": bf(np.random.standard_normal((N, H)) * u[:, None]),
              "x": bf(np.random.standard_normal((N, D)) * u[:, None])}
    uc = np.random.standard_normal((H, H)) / np.sqrt(H) / s[None, :]
    words, scales = pack4(uc.T)
    inputs["uc_words"] = words
    inputs["uc_scales"] = scales
    return inputs


def candidate_preact_grad(g, z, c):
    return g * (1.0 - z) * (1.0 - c * c)


def reset_preact_grad(da, h, r):
    return da * h * r * (1.0 - r)


def core(g, z, c, r, h, x, uc_words, uc_scales):
    e = candidate_preact_grad(f64(g), f64(z), f64(c))
    da = mxq(e, 1, "e4m3") @ unpack4(uc_words, uc_scales)
    dr = reset_preact_grad(da, f64(h), f64(r))
    drq = mxq(dr, 0, "e4m3")
    dur = mxq(f64(h), 0, "e4m3").T @ drq
    dwr = mxq(f64(x), 0, "e4m3").T @ drq
    return dur, dwr


def e4m3fn_bytes(y):
    return np.clip(np.asarray(y, np.float64), -448.0, 448.0).astype(np.float32).astype(ml_dtypes.float8_e4m3fn).view(np.uint8)


def e4m3fn_values(b):
    return np.asarray(b, np.uint8).view(ml_dtypes.float8_e4m3fn).astype(np.float64)


def setup_inputs():
    d = draw0()
    x0 = np.asarray(d['x']).astype(np.float64)
    s = (np.max(np.abs(x0), axis=(1,), keepdims=True) / 448.0).astype(np.float32)
    out = {}
    for k, v in d.items():
        if k == 'x':
            out['x_bytes'] = e4m3fn_bytes(x0 / s.astype(np.float64))
            out['x_scale'] = s
        else:
            out[k] = v
    return out


def reference(g, z, c, r, h, x_bytes, x_scale, uc_words, uc_scales):
    return core(g, z, c, r, h, e4m3fn_values(x_bytes) * x_scale.astype(np.float64), uc_words, uc_scales)

@@ -1,0 +1,491 @@
+from contextlib import ExitStack
+
+import concourse.mybir as mybir
+from concourse.masks import make_identity
+
+F32 = mybir.dt.float32
+BF16 = mybir.dt.bfloat16
+I32 = mybir.dt.int32
+U32 = mybir.dt.uint32
+U8 = mybir.dt.uint8
+FP8 = mybir.dt.float8_e4m3fn
+FP8X4 = mybir.dt.float8_e4m3fn_x4
+FP4X4 = mybir.dt.float4_e2m1fn_x4
+ALU = mybir.AluOpType
+ACT = mybir.ActivationFunctionType
+
+P = 128
+N = 1024
+FLOPS = 3 * 2 * N * N * N
+CH = 256
+V, S, G = "v", "s", "g"
+
+
+def tile_gruresetgateweightgradient_w4_kernel(tc, g, z, c, r, h, x_bytes, x_scale, uc_words, uc_scales, out_0, out_1):
+    nc = tc.nc
+    with ExitStack() as ctx:
+        keep = ctx.enter_context(tc.tile_pool(name="keep", bufs=1))
+        pool = ctx.enter_context(tc.tile_pool(name="pool", bufs=2))
+        psum = ctx.enter_context(tc.psum_pool(name="psum", bufs=4))
+
+        id_f = keep.tile([P, P], F32, name="id_f")
+        id_b = keep.tile([P, P], BF16, name="id_b")
+        ucw = keep.tile([P, 2, 2 * N], U8, align_bytes=64, name="ucw")
+        ucs = keep.tile([P, 2, N], U8, align_bytes=64, name="ucs")
+        xs = keep.tile([P, 2, 4], F32, name="xs")
+        zero = keep.tile([P, 1], F32, name="zero")
+        make_identity(nc, id_f[:])
+        make_identity(nc, id_b[:])
+
+        def rows(ap):
+            return ap.rearrange("(g p t) i -> g p t i", g=2, p=P, t=4)
+
+        gz, gg, gc, gr, gh = rows(z), rows(g), rows(c), rows(r), rows(h)
+        xv = x_bytes.rearrange("(g p t) i -> g p (t i)", g=2, p=P, t=4)
+
+        zt, gt, ct = {}, {}, {}
+
+        def load_zgc(nm, pi, t):
+            d, src = {"z": (zt, gz), "g": (gt, gg), "c": (ct, gc)}[nm]
+            gi, tp = divmod(pi, 2)
+            if pi not in d:
+                d[pi] = pool.tile([P, 2, N], BF16, tag="ld", bufs=8, name=nm + str(pi))
+            lo, hi = (0, 2) if t is None else (t, t + 1)
+            nc.sync.dma_start(out=d[pi][:, lo:hi, :], in_=src[gi][:, 2 * tp + lo : 2 * tp + hi, :])
+
+        def load_uw():
+            nc.sync.dma_start(out=ucw[:], in_=uc_words.rearrange("k p n -> p k n"))
+
+        def load_us(q):
+            nc.sync.dma_start(out=ucs[32 * q : 32 * q + 4, :, :].bitcast(I32), in_=uc_scales[:, 4 * q : 4 * q + 4, :].rearrange("k q n -> q k n").bitcast(I32))
+
+        def load_xs():
+            nc.sync.dma_start(out=xs[:], in_=x_scale.rearrange("(g p t) o -> p g (t o)", g=2, p=P, t=4))
+
+        quad = {}
+
+        def load_quad(nm, gi):
+            src = gh if nm == "h" else gr
+            quad[nm, gi] = pool.tile([P, 4, N], BF16, tag="q4", bufs=6, name=nm + str(gi))
+            nc.sync.dma_start(out=quad[nm, gi][:], in_=src[gi])
+
+        def copy(eng, out, in_):
+            if eng == V:
+                nc.vector.tensor_copy(out=out, in_=in_)
+            else:
+                nc.scalar.copy(out=out, in_=in_)
+
+        c2, av, eb, xt, eg, ec, es = {}, {}, {}, {}, {}, {}, {}
+
+        def sq(pi, t):
+            c2[pi, t] = pool.tile([P, N], F32, tag="c2", bufs=3, name="c2_%d%d" % (pi, t))
+            nc.scalar.activation(out=c2[pi, t][:], in_=ct[pi][:, t, :], func=ACT.Square)
+
+        def s1(pi, t):
+            av[pi, t] = pool.tile([P, N], F32, tag="av", bufs=3, name="a_%d%d" % (pi, t))
+            nc.vector.scalar_tensor_tensor(out=av[pi, t][:], in0=zt[pi][:, t, :], scalar=1.0, in1=gt[pi][:, t, :], op0=ALU.subtract, op1=ALU.mult)
+
+        def s2(pi, t):
+            eb[pi, t] = pool.tile([P, N], BF16, tag="eb", bufs=4, align_bytes=64, name="e_%d%d" % (pi, t))
+            nc.vector.scalar_tensor_tensor(out=eb[pi, t][:], in0=c2[pi, t][:], scalar=1.0, in1=av[pi, t][:], op0=ALU.subtract, op1=ALU.mult)
+
+        def tr(pi, t):
+            xt[pi, t] = psum.tile([P, 2, 2, P], F32, tag="mm", bufs=3, name="xt_%d%d" % (pi, t))
+            words = eb[pi, t][:].bitcast(F32)
+            for k in range(2):
+                for u in range(2):
+                    nc.tensor.transpose(xt[pi, t][:, k, u, :], words[:, 256 * k + u : 256 * (k + 1) : 2], id_f[:])
+
+        def tcp(pi, t, eng):
+            if pi not in eg:
+                eg[pi] = pool.tile([P, 2 * 2 * P * 4], BF16, tag="eg", bufs=2, align_bytes=64, name="eg_%d" % pi)
+            dst = eg[pi][:].bitcast(F32)[:, 512 * t : 512 * (t + 1)].rearrange("p (k m u) -> p k m u", k=2, u=2)
+            copy(eng, dst, xt[pi, t][:].rearrange("p k u m -> p k m u"))
+
+        def qe(pi):
+            ec[pi] = keep.tile([P, 512], U32, align_bytes=64, name="ec_%d" % pi)
+            es[pi] = keep.tile([P, 512], U8, align_bytes=64, name="es_%d" % pi)
+            nc.vector.quantize_mx(out=ec[pi][:].bitcast(FP8X4), scales=es[pi][:], in_=eg[pi][:])
+
+        il = {}
+
+        def pe_h(gi, half, j):
+            bank = psum.tile([P, 2 * 512], BF16, tag="mm", bufs=3, name="il_%d%d%d" % (gi, half, j))
+            il[gi, half, j] = bank
+            for k in range(2):
+                c0 = 512 * half + 256 * j + 128 * k
+                nc.tensor.matmul(
+                    bank[:, 512 * k : 512 * (k + 1)].rearrange("p (n t) -> p n t", t=4),
+                    lhsT=id_b[:],
+                    rhs=quad["h", gi][:, :, c0 : c0 + 128].rearrange("p t n -> p n t"),
+                    start=True, stop=True)
+
+        ht = {}
+
+        def h_cp(gi, half, j, eng):
+            if ("h", gi, half) not in ht:
+                ht["h", gi, half] = pool.tile([P, 512, 4], BF16, tag="il", bufs=3, align_bytes=64, name="ilt_h%d%d" % (gi, half))
+            copy(eng, ht["h", gi, half][:, 256 * j : 256 * (j + 1), :].rearrange("p n t -> p (n t)"), il[gi, half, j][:])
+
+        def x_il(gi, half, eng):
+            ht["x", gi, half] = pool.tile([P, 512, 4], BF16, tag="il", bufs=3, align_bytes=64, name="ilt_x%d%d" % (gi, half))
+            src = quad["x", gi][:, :, 512 * half : 512 * (half + 1)].rearrange("p t n -> p n t")
+            if eng == V:
+                nc.vector.tensor_copy(out=ht["x", gi, half][:], in_=src)
+            else:
+                nc.scalar.copy(out=ht["x", gi, half][:], in_=src)
+
+        rb = {}
+
+        def pe_r(gi, b):
+            bank = psum.tile([P, 2 * 512], BF16, tag="rb", bufs=2, name="rb_%d%d" % (gi, b))
+            rb[gi, b] = bank
+            for k in range(2):
+                c0 = CH * b + 128 * k
+                nc.tensor.matmul(
+                    bank[:, 512 * k : 512 * (k + 1)].rearrange("p (n t) -> p n t", t=4),
+                    lhsT=id_b[:],
+                    rhs=quad["r", gi][:, :, c0 : c0 + 128].rearrange("p t n -> p n t"),
+                    start=True, stop=True)
+
+        qc, qs = {}, {}
+
+        def q_w(nm, gi, half):
+            if (nm, gi) not in qc:
+                qc[nm, gi] = keep.tile([P, N], U32, align_bytes=64, name="qc_%s%d" % (nm, gi))
+                qs[nm, gi] = keep.tile([P, N], U8, align_bytes=64, name="qs_%s%d" % (nm, gi))
+            sl = slice(512 * half, 512 * (half + 1))
+            nc.vector.quantize_mx(out=qc[nm, gi][:, sl].bitcast(FP8X4), scales=qs[nm, gi][:, sl], in_=ht[nm, gi, half][:].rearrange("p n t -> p (n t)"))
+
+        xb = {}
+
+        def load_x(gi):
+            xb[gi] = keep.tile([P, 4 * N], U8, align_bytes=64, name="xb_%d" % gi)
+            nc.sync.dma_start(out=xb[gi][:], in_=xv[gi])
+
+        def widen(gi, t, eng):
+            if ("x", gi) not in quad:
+                quad["x", gi] = pool.tile([P, 4, N], BF16, tag="q4", bufs=6, name="x" + str(gi))
+            src = xb[gi][:, N * t : N * (t + 1)].bitcast(FP8)
+            if eng == V:
+                nc.vector.tensor_scalar(out=quad["x", gi][:, t, :], in0=src, scalar1=xs[:, gi, t : t + 1], scalar2=None, op0=ALU.mult)
+            else:
+                nc.scalar.activation(out=quad["x", gi][:, t, :], in_=src, func=ACT.Copy, scale=xs[:, gi, t : t + 1])
+
+        w, hr = {}, {}
+
+        def hxr(gi, b, eng):
+            hr[gi, b] = pool.tile([P, CH, 4], F32, tag="hr", bufs=2, name="hr_%d%d" % (gi, b))
+            sl = slice(CH * b, CH * (b + 1))
+            e = nc.vector if eng == V else nc.gpsimd
+            e.tensor_tensor(out=hr[gi, b][:], in0=quad["h", gi][:, :, sl].rearrange("p t n -> p n t"), in1=quad["r", gi][:, :, sl].rearrange("p t n -> p n t"), op=ALU.mult)
+
+        def wop(gi, b):
+            w[gi, b] = pool.tile([P, CH, 4], F32, tag="w", bufs=4, name="w_%d%d" % (gi, b))
+            nc.vector.scalar_tensor_tensor(out=w[gi, b][:].rearrange("p n t -> p (n t)"), in0=rb[gi, b][:], scalar=1.0, in1=hr[gi, b][:].rearrange("p n t -> p (n t)"), op0=ALU.subtract, op1=ALU.mult)
+
+        da = {}
+
+        def pe_da(b, gi, j):
+            bank = psum.tile([P, 4, P], F32, tag="da", bufs=3, name="da_%d%d%d" % (b, gi, j))
+            da[b, gi, j] = bank
+            i0 = CH * b + P * j
+            for t in range(4):
+                pi = 2 * gi + t // 2
+                for k in range(2):
+                    o = P * (2 * (t % 2) + k)
+                    nc.tensor.matmul_mx(
+                        out=bank[:, t, :],
+                        lhsT=ec[pi][:, o : o + P].bitcast(FP8X4), lhsT_scale=es[pi][:, o : o + P],
+                        rhs=ucw[:, k, 2 * i0 : 2 * (i0 + P)].bitcast(FP4X4), rhs_scale=ucs[:, k, i0 : i0 + P],
+                        start=(k == 0), stop=(k == 1))
+
+        dr, dc, ds = {}, {}, {}
+
+        def drop(b, gi, j):
+            if b not in dr:
+                dr[b] = pool.tile([P, 2, CH, 4], BF16, tag="dr", bufs=2, align_bytes=64, name="dr_%d" % b)
+            nc.vector.scalar_tensor_tensor(out=dr[b][:, gi, P * j : P * (j + 1), :], in0=da[b, gi, j][:].rearrange("p t n -> p n t"), scalar=-1.0, in1=w[gi, b][:, P * j : P * (j + 1), :], op0=ALU.mult, op1=ALU.mult)
+
+        def qdr(b):
+            dc[b] = keep.tile([P, 2, CH], U32, align_bytes=64, name="dc_%d" % b)
+            ds[b] = keep.tile([P, 2, CH], U8, align_bytes=64, name="ds_%d" % b)
+            nc.vector.quantize_mx(out=dc[b][:].rearrange("p g n -> p (g n)").bitcast(FP8X4), scales=ds[b][:].rearrange("p g n -> p (g n)"), in_=dr[b][:].rearrange("p g n t -> p (g n t)"))
+
+        res = {}
+
+        obank = {}
+
+        def o_mm(nm, b, q):
+            bank = psum.tile([P, 2, CH], F32, tag="mm", bufs=3, name="o_%s%d%d" % (nm, b, q))
+            obank[nm, b, q] = bank
+            for m in range(2):
+                m0 = P * (2 * q + m)
+                for gi in range(2):
+                    nc.tensor.matmul_mx(
+                        out=bank[:, m, :],
+                        lhsT=qc[nm, gi][:, m0 : m0 + P].bitcast(FP8X4), lhsT_scale=qs[nm, gi][:, m0 : m0 + P],
+                        rhs=dc[b][:, gi, :].bitcast(FP8X4), rhs_scale=ds[b][:, gi, :],
+                        start=(gi == 0), stop=(gi == 1))
+
+        def o_cp(nm, b, q, eng):
+            if (nm, b, q // 2) not in res:
+                res[nm, b, q // 2] = pool.tile([P, 4, CH], F32, tag="out", bufs=4, name="r_%s%d%d" % (nm, b, q // 2))
+            copy(eng, res[nm, b, q // 2][:, 2 * (q % 2) : 2 * (q % 2) + 2, :], obank[nm, b, q][:])
+
+        def o_st(nm, b, q2):
+            dst = out_0 if nm == "h" else out_1
+            r0 = 512 * q2
+            nc.sync.dma_start(out=dst[r0 : r0 + 512, CH * b : CH * (b + 1)].rearrange("(m p) i -> p m i", p=P), in_=res[nm, b, q2][:])
+
+        nc.gpsimd.memset(zero[:], 0.0)
+        nc.gpsimd.memset(ucs[:].rearrange("p k n -> p (k n)").bitcast(U32), 0)
+        with tc.manual_schedule():
+            nc.scalar.activation(out=zero[:], in_=zero[:], func=ACT.Square)
+            load_zgc("c", 0, 0)
+            load_zgc("c", 0, 1)
+            load_zgc("g", 0, 0)
+            sq(0, 1)
+            load_zgc("z", 0, 0)
+            load_zgc("g", 1, None)
+            load_xs()
+            load_zgc("z", 0, 1)
+            s1(0, 0)
+            sq(0, 0)
+            s2(0, 0)
+            load_zgc("g", 0, 1)
+            load_zgc("z", 1, None)
+            s1(0, 1)
+            load_zgc("c", 1, None)
+            s1(1, 1)
+            load_zgc("c", 2, None)
+            tr(0, 0)
+            s2(0, 1)
+            load_zgc("z", 2, None)
+            s1(1, 0)
+            sq(1, 1)
+            load_zgc("g", 2, None)
+            sq(1, 0)
+            s2(1, 1)
+            tcp(0, 0, S)
+            tr(0, 1)
+            s1(2, 1)
+            sq(2, 0)
+            tcp(0, 1, S)
+            load_zgc("g", 3, None)
+            sq(2, 1)
+            s2(1, 0)
+            load_zgc("z", 3, None)
+            load_x(0)
+            tr(1, 0)
+            s1(2, 0)
+            s2(2, 1)
+            load_zgc("c", 3, None)
+            tr(1, 1)
+            load_quad("r", 0)
+            s2(2, 0)
+            widen(0, 0, S)
+            tr(2, 1)
+            tcp(1, 1, S)
+            s1(3, 0)
+            tcp(1, 0, S)
+            tr(2, 0)
+            load_quad("h", 0)
+            sq(3, 0)
+            qe(1)
+            widen(0, 2, S)
+            sq(3, 1)
+            qe(0)
+            tcp(2, 1, S)
+            s2(3, 0)
+            load_quad("r", 1)
+            pe_h(0, 0, 0)
+            tr(3, 0)
+            pe_r(0, 0)
+            pe_r(1, 0)
+            s1(3, 1)
+            widen(0, 1, S)
+            tcp(2, 0, S)
+            s2(3, 1)
+            tr(3, 1)
+            load_quad("h", 1)
+            tcp(3, 0, S)
+            load_x(1)
+            h_cp(0, 0, 0, S)
+            qe(2)
+            load_uw()
+            hxr(0, 0, G)
+            wop(0, 0)
+            pe_h(0, 1, 1)
+            load_us(3)
+            load_us(2)
+            tcp(3, 1, S)
+            load_us(1)
+            pe_h(0, 0, 1)
+            h_cp(0, 1, 1, S)
+            qe(3)
+            pe_h(0, 1, 0)
+            pe_h(1, 0, 1)
+            widen(1, 3, V)
+            h_cp(0, 0, 1, S)
+            h_cp(0, 1, 0, S)
+            q_w("h", 0, 1)
+            pe_r(0, 1)
+            load_us(0)
+            widen(0, 3, S)
+            hxr(1, 0, G)
+            pe_h(1, 0, 0)
+            wop(1, 0)
+            pe_da(0, 0, 1)
+            q_w("h", 0, 0)
+            pe_da(0, 0, 0)
+            drop(0, 0, 1)
+            drop(0, 0, 0)
+            widen(1, 2, S)
+            pe_h(1, 1, 0)
+            h_cp(1, 0, 0, S)
+            h_cp(1, 0, 1, S)
+            pe_r(1, 1)
+            hxr(0, 1, G)
+            h_cp(1, 1, 0, S)
+            hxr(1, 1, G)
+            wop(0, 1)
+            pe_da(0, 1, 0)
+            drop(0, 1, 0)
+            pe_da(1, 0, 0)
+            q_w("h", 1, 0)
+            pe_da(0, 1, 1)
+            drop(0, 1, 1)
+            x_il(0, 1, S)
+            pe_r(0, 2)
+            x_il(0, 0, S)
+            wop(1, 1)
+            qdr(0)
+            pe_h(1, 1, 1)
+            pe_da(1, 0, 1)
+            o_mm("h", 0, 1)
+            h_cp(1, 1, 1, S)
+            drop(1, 0, 0)
+            hxr(0, 2, G)
+            drop(1, 0, 1)
+            o_mm("h", 0, 0)
+            pe_da(1, 1, 0)
+            pe_da(1, 1, 1)
+            pe_da(2, 0, 0)
+            widen(1, 1, V)
+            q_w("h", 1, 1)
+            o_mm("h", 0, 2)
+            drop(1, 1, 0)
+            drop(1, 1, 1)
+            pe_r(1, 2)
+            o_cp("h", 0, 1, S)
+            q_w("x", 0, 1)
+            o_cp("h", 0, 0, S)
+            qdr(1)
+            o_cp("h", 0, 2, V)
+            widen(1, 0, S)
+            wop(0, 2)
+            pe_da(2, 0, 1)
+            q_w("x", 0, 0)
+            o_mm("h", 1, 0)
+            x_il(1, 0, S)
+            o_st("h", 0, 0)
+            o_mm("h", 0, 3)
+            o_cp("h", 1, 0, S)
+            o_cp("h", 0, 3, S)
+            pe_da(2, 1, 0)
+            q_w("x", 1, 0)
+            o_mm("h", 1, 2)
+            o_mm("h", 1, 1)
+            o_cp("h", 1, 1, S)
+            drop(2, 0, 0)
+            x_il(1, 1, V)
+            o_cp("h", 1, 2, S)
+            o_mm("h", 1, 3)
+            pe_da(2, 1, 1)
+            q_w("x", 1, 1)
+            pe_r(0, 3)
+            o_mm("x", 0, 0)
+            hxr(1, 2, G)
+            o_st("h", 0, 1)
+            wop(1, 2)
+            o_cp("h", 1, 3, S)
+            o_mm("x", 0, 1)
+            o_st("h", 1, 0)
+            drop(2, 0, 1)
+            o_cp("x", 0, 0, S)
+            drop(2, 1, 1)
+            o_mm("x", 0, 3)
+            o_cp("x", 0, 1, S)
+            o_cp("x", 0, 3, S)
+            o_st("h", 1, 1)
+            o_mm("x", 0, 2)
+            hxr(0, 3, G)
+            drop(2, 1, 0)
+            o_cp("x", 0, 2, S)
+            o_st("x", 0, 0)
+            qdr(2)
+            o_mm("x", 1, 1)
+            pe_da(3, 0, 0)
+            o_mm("x", 1, 2)
+            o_mm("x", 1, 0)
+            o_cp("x", 1, 1, S)
+            o_cp("x", 1, 0, V)
+            o_cp("x", 1, 2, S)
+            o_mm("x", 1, 3)
+            o_cp("x", 1, 3, S)
+            pe_r(1, 3)
+            o_mm("h", 2, 1)
+            hxr(1, 3, G)
+            wop(0, 3)
+            o_mm("h", 2, 0)
+            o_cp("h", 2, 0, S)
+            pe_da(3, 1, 1)
+            o_st("x", 0, 1)
+            o_st("x", 1, 0)
+            pe_da(3, 0, 1)
+            wop(1, 3)
+            o_cp("h", 2, 1, V)
+            o_st("x", 1, 1)
+            o_mm("h", 2, 2)
+            drop(3, 1, 1)
+            o_cp("h", 2, 2, S)
+            o_st("h", 2, 0)
+            o_mm("h", 2, 3)
+            o_mm("x", 2, 1)
+            o_cp("h", 2, 3, S)
+            drop(3, 0, 0)
+            pe_da(3, 1, 0)
+            drop(3, 0, 1)
+            drop(3, 1, 0)
+            qdr(3)
+            o_cp("x", 2, 1, S)
+            o_mm("x", 2, 0)
+            o_mm("x", 2, 3)
+            o_st("h", 2, 1)
+            o_mm("x", 2, 2)
+            o_cp("x", 2, 0, S)
+            o_mm("h", 3, 0)
+            o_cp("x", 2, 3, S)
+            o_cp("x", 2, 2, S)
+            o_cp("h", 3, 0, V)
+            o_mm("h", 3, 1)
+            o_mm("h", 3, 3)
+            o_cp("h", 3, 1, V)
+            o_mm("h", 3, 2)
+            o_st("x", 2, 0)
+            o_st("x", 2, 1)
+            o_mm("x", 3, 0)
+            o_cp("h", 3, 2, V)
+            o_cp("h", 3, 3, S)
+            o_cp("x", 3, 0, V)
+            o_st("h", 3, 0)
+            o_mm("x", 3, 1)
+            o_mm("x", 3, 2)
+            o_mm("x", 3, 3)
+            o_cp("x", 3, 1, S)
+            o_cp("x", 3, 2, S)
+            o_st("h", 3, 1)
+            o_st("x", 3, 0)
+            o_cp("x", 3, 3, V)
+            o_st("x", 3, 1)

@@ -66,7 +66,7 @@ def tile_gruresetgateweightgradient_w4_kernel(tc, g, z, c, r, h, x_bytes, x_scal
 
         def load_quad(nm, gi):
             src = gh if nm == "h" else gr
-            quad[nm, gi] = pool.tile([P, 4, N], BF16, tag="q4", bufs=6, name=nm + str(gi))
+            quad[nm, gi] = pool.tile([P, 4, N], BF16, tag="q4" if nm == "h" else "r4", bufs=3 if nm == "h" else 2, name=nm + str(gi))
             nc.sync.dma_start(out=quad[nm, gi][:], in_=src[gi])
 
         def copy(eng, out, in_):
@@ -90,7 +90,7 @@ def tile_gruresetgateweightgradient_w4_kernel(tc, g, z, c, r, h, x_bytes, x_scal
             nc.vector.scalar_tensor_tensor(out=eb[pi, t][:], in0=c2[pi, t][:], scalar=1.0, in1=av[pi, t][:], op0=ALU.subtract, op1=ALU.mult)
 
         def tr(pi, t):
-            xt[pi, t] = psum.tile([P, 2, 2, P], F32, tag="mm", bufs=3, name="xt_%d%d" % (pi, t))
+            xt[pi, t] = psum.tile([P, 2, 2, P], F32, tag="mm", bufs=4, name="xt_%d%d" % (pi, t))
             words = eb[pi, t][:].bitcast(F32)
             for k in range(2):
                 for u in range(2):
@@ -109,44 +109,23 @@ def tile_gruresetgateweightgradient_w4_kernel(tc, g, z, c, r, h, x_bytes, x_scal
 
         il = {}
 
-        def pe_h(gi, half, j):
-            bank = psum.tile([P, 2 * 512], BF16, tag="mm", bufs=3, name="il_%d%d%d" % (gi, half, j))
-            il[gi, half, j] = bank
+        def pe_il(nm, gi, half, j):
+            bank = psum.tile([P, 2 * 512], BF16, tag="mm", bufs=4, name="il_%s%d%d%d" % (nm, gi, half, j))
+            il[nm, gi, half, j] = bank
             for k in range(2):
                 c0 = 512 * half + 256 * j + 128 * k
                 nc.tensor.matmul(
                     bank[:, 512 * k : 512 * (k + 1)].rearrange("p (n t) -> p n t", t=4),
                     lhsT=id_b[:],
-                    rhs=quad["h", gi][:, :, c0 : c0 + 128].rearrange("p t n -> p n t"),
+                    rhs=quad[nm, gi][:, :, c0 : c0 + 128].rearrange("p t n -> p n t"),
                     start=True, stop=True)
 
         ht = {}
 
-        def h_cp(gi, half, j, eng):
-            if ("h", gi, half) not in ht:
-                ht["h", gi, half] = pool.tile([P, 512, 4], BF16, tag="il", bufs=3, align_bytes=64, name="ilt_h%d%d" % (gi, half))
-            copy(eng, ht["h", gi, half][:, 256 * j : 256 * (j + 1), :].rearrange("p n t -> p (n t)"), il[gi, half, j][:])
-
-        def x_il(gi, half, eng):
-            ht["x", gi, half] = pool.tile([P, 512, 4], BF16, tag="il", bufs=3, align_bytes=64, name="ilt_x%d%d" % (gi, half))
-            src = quad["x", gi][:, :, 512 * half : 512 * (half + 1)].rearrange("p t n -> p n t")
-            if eng == V:
-                nc.vector.tensor_copy(out=ht["x", gi, half][:], in_=src)
-            else:
-                nc.scalar.copy(out=ht["x", gi, half][:], in_=src)
-
-        rb = {}
-
-        def pe_r(gi, b):
-            bank = psum.tile([P, 2 * 512], BF16, tag="rb", bufs=2, name="rb_%d%d" % (gi, b))
-            rb[gi, b] = bank
-            for k in range(2):
-                c0 = CH * b + 128 * k
-                nc.tensor.matmul(
-                    bank[:, 512 * k : 512 * (k + 1)].rearrange("p (n t) -> p n t", t=4),
-                    lhsT=id_b[:],
-                    rhs=quad["r", gi][:, :, c0 : c0 + 128].rearrange("p t n -> p n t"),
-                    start=True, stop=True)
+        def il_cp(nm, gi, half, j, eng):
+            if (nm, gi, half) not in ht:
+                ht[nm, gi, half] = pool.tile([P, 512, 4], BF16, tag="il" + nm, bufs=2 if nm == "x" else 4, align_bytes=64, name="ilt_%s%d%d" % (nm, gi, half))
+            copy(eng, ht[nm, gi, half][:, 256 * j : 256 * (j + 1), :].rearrange("p n t -> p (n t)"), il[nm, gi, half, j][:])
 
         qc, qs = {}, {}
 
@@ -165,29 +144,28 @@ def tile_gruresetgateweightgradient_w4_kernel(tc, g, z, c, r, h, x_bytes, x_scal
 
         def widen(gi, t, eng):
             if ("x", gi) not in quad:
-                quad["x", gi] = pool.tile([P, 4, N], BF16, tag="q4", bufs=6, name="x" + str(gi))
+                quad["x", gi] = pool.tile([P, 4, N], BF16, tag="q4", bufs=3, name="x" + str(gi))
             src = xb[gi][:, N * t : N * (t + 1)].bitcast(FP8)
             if eng == V:
                 nc.vector.tensor_scalar(out=quad["x", gi][:, t, :], in0=src, scalar1=xs[:, gi, t : t + 1], scalar2=None, op0=ALU.mult)
             else:
                 nc.scalar.activation(out=quad["x", gi][:, t, :], in_=src, func=ACT.Copy, scale=xs[:, gi, t : t + 1])
 
-        w, hr = {}, {}
+        w = {}
 
-        def hxr(gi, b, eng):
-            hr[gi, b] = pool.tile([P, CH, 4], F32, tag="hr", bufs=2, name="hr_%d%d" % (gi, b))
-            sl = slice(CH * b, CH * (b + 1))
-            e = nc.vector if eng == V else nc.gpsimd
-            e.tensor_tensor(out=hr[gi, b][:], in0=quad["h", gi][:, :, sl].rearrange("p t n -> p n t"), in1=quad["r", gi][:, :, sl].rearrange("p t n -> p n t"), op=ALU.mult)
+        def t1(gi, b):
+            w[gi, b] = pool.tile([P, CH, 4], F32, tag="w", bufs=4, name="w_%d%d" % (gi, b))
+            rr = quad["r", gi][:, :, CH * b : CH * (b + 1)].rearrange("p t n -> p n t")
+            nc.vector.scalar_tensor_tensor(out=w[gi, b][:], in0=rr, scalar=1.0, in1=rr, op0=ALU.subtract, op1=ALU.mult)
 
         def wop(gi, b):
-            w[gi, b] = pool.tile([P, CH, 4], F32, tag="w", bufs=4, name="w_%d%d" % (gi, b))
-            nc.vector.scalar_tensor_tensor(out=w[gi, b][:].rearrange("p n t -> p (n t)"), in0=rb[gi, b][:], scalar=1.0, in1=hr[gi, b][:].rearrange("p n t -> p (n t)"), op0=ALU.subtract, op1=ALU.mult)
+            o = CH * (b % 2)
+            nc.vector.tensor_tensor(out=w[gi, b][:], in0=w[gi, b][:], in1=ht["h", gi, b // 2][:, o : o + CH, :], op=ALU.mult)
 
         da = {}
 
         def pe_da(b, gi, j):
-            bank = psum.tile([P, 4, P], F32, tag="da", bufs=3, name="da_%d%d%d" % (b, gi, j))
+            bank = psum.tile([P, 4, P], F32, tag="da", bufs=4, name="da_%d%d%d" % (b, gi, j))
             da[b, gi, j] = bank
             i0 = CH * b + P * j
             for t in range(4):
@@ -217,7 +195,7 @@ def tile_gruresetgateweightgradient_w4_kernel(tc, g, z, c, r, h, x_bytes, x_scal
         obank = {}
 
         def o_mm(nm, b, q):
-            bank = psum.tile([P, 2, CH], F32, tag="mm", bufs=3, name="o_%s%d%d" % (nm, b, q))
+            bank = psum.tile([P, 2, CH], F32, tag="mm", bufs=4, name="o_%s%d%d" % (nm, b, q))
             obank[nm, b, q] = bank
             for m in range(2):
                 m0 = P * (2 * q + m)
@@ -242,250 +220,254 @@ def tile_gruresetgateweightgradient_w4_kernel(tc, g, z, c, r, h, x_bytes, x_scal
         nc.gpsimd.memset(ucs[:].rearrange("p k n -> p (k n)").bitcast(U32), 0)
         with tc.manual_schedule():
             nc.scalar.activation(out=zero[:], in_=zero[:], func=ACT.Square)
-            load_zgc("c", 0, 0)
-            load_zgc("c", 0, 1)
-            load_zgc("g", 0, 0)
-            sq(0, 1)
-            load_zgc("z", 0, 0)
-            load_zgc("g", 1, None)
-            load_xs()
             load_zgc("z", 0, 1)
+            load_zgc("z", 0, 0)
+            load_zgc("g", 0, 1)
+            load_zgc("c", 0, 1)
+            s1(0, 1)
+            sq(0, 1)
+            load_zgc("g", 0, 0)
+            load_zgc("c", 0, 0)
+            load_zgc("z", 1, None)
             s1(0, 0)
+            s2(0, 1)
+            tr(0, 1)
             sq(0, 0)
             s2(0, 0)
-            load_zgc("g", 0, 1)
-            load_zgc("z", 1, None)
-            s1(0, 1)
+            load_zgc("g", 1, None)
             load_zgc("c", 1, None)
-            s1(1, 1)
-            load_zgc("c", 2, None)
-            tr(0, 0)
-            s2(0, 1)
-            load_zgc("z", 2, None)
-            s1(1, 0)
-            sq(1, 1)
             load_zgc("g", 2, None)
-            sq(1, 0)
-            s2(1, 1)
-            tcp(0, 0, S)
-            tr(0, 1)
-            s1(2, 1)
-            sq(2, 0)
             tcp(0, 1, S)
-            load_zgc("g", 3, None)
-            sq(2, 1)
-            s2(1, 0)
-            load_zgc("z", 3, None)
-            load_x(0)
-            tr(1, 0)
-            s1(2, 0)
-            s2(2, 1)
+            s1(1, 0)
+            tr(0, 0)
+            sq(1, 0)
+            load_zgc("z", 2, None)
+            s1(1, 1)
             load_zgc("c", 3, None)
-            tr(1, 1)
-            load_quad("r", 0)
-            s2(2, 0)
-            widen(0, 0, S)
-            tr(2, 1)
-            tcp(1, 1, S)
-            s1(3, 0)
-            tcp(1, 0, S)
-            tr(2, 0)
+            s2(1, 0)
+            load_zgc("c", 2, None)
+            s1(2, 0)
+            load_zgc("z", 3, None)
+            sq(1, 1)
+            tr(1, 0)
+            load_zgc("g", 3, None)
             load_quad("h", 0)
+            pe_il("h", 0, 1, 1)
+            load_xs()
+            load_us(0)
+            load_us(1)
+            load_us(2)
+            load_us(3)
+            load_uw()
+            load_quad("r", 0)
+            s1(2, 1)
+            sq(2, 1)
+            sq(2, 0)
+            s2(1, 1)
+            tcp(1, 0, S)
+            pe_il("h", 0, 0, 1)
+            s2(2, 1)
+            tcp(0, 0, S)
+            load_x(0)
+            pe_il("h", 0, 0, 0)
+            load_quad("h", 1)
             sq(3, 0)
-            qe(1)
-            widen(0, 2, S)
+            s1(3, 0)
+            tr(1, 1)
+            s2(2, 0)
             sq(3, 1)
+            s1(3, 1)
+            il_cp("h", 0, 0, 1, S)
+            tcp(1, 1, S)
+            il_cp("h", 0, 0, 0, S)
             qe(0)
-            tcp(2, 1, S)
+            il_cp("h", 0, 1, 1, S)
             s2(3, 0)
             load_quad("r", 1)
-            pe_h(0, 0, 0)
+            widen(0, 2, S)
+            t1(0, 0)
             tr(3, 0)
-            pe_r(0, 0)
-            pe_r(1, 0)
-            s1(3, 1)
-            widen(0, 1, S)
-            tcp(2, 0, S)
-            s2(3, 1)
-            tr(3, 1)
-            load_quad("h", 1)
+            qe(1)
             tcp(3, 0, S)
-            load_x(1)
-            h_cp(0, 0, 0, S)
-            qe(2)
-            load_uw()
-            hxr(0, 0, G)
-            wop(0, 0)
-            pe_h(0, 1, 1)
-            load_us(3)
-            load_us(2)
-            tcp(3, 1, S)
-            load_us(1)
-            pe_h(0, 0, 1)
-            h_cp(0, 1, 1, S)
-            qe(3)
-            pe_h(0, 1, 0)
-            pe_h(1, 0, 1)
-            widen(1, 3, V)
-            h_cp(0, 0, 1, S)
-            h_cp(0, 1, 0, S)
-            q_w("h", 0, 1)
-            pe_r(0, 1)
-            load_us(0)
-            widen(0, 3, S)
-            hxr(1, 0, G)
-            pe_h(1, 0, 0)
-            wop(1, 0)
-            pe_da(0, 0, 1)
             q_w("h", 0, 0)
+            widen(0, 3, S)
+            tr(2, 0)
+            s2(3, 1)
+            pe_il("h", 1, 0, 0)
+            widen(0, 0, S)
+            tcp(2, 0, S)
+            tr(2, 1)
+            tr(3, 1)
+            il_cp("h", 1, 0, 0, S)
+            tcp(2, 1, S)
+            wop(0, 0)
+            pe_il("h", 1, 1, 1)
+            load_x(1)
+            t1(0, 1)
+            widen(0, 1, S)
+            t1(1, 0)
+            tcp(3, 1, S)
+            pe_il("h", 0, 1, 0)
+            pe_il("h", 1, 1, 0)
+            qe(2)
             pe_da(0, 0, 0)
-            drop(0, 0, 1)
-            drop(0, 0, 0)
-            widen(1, 2, S)
-            pe_h(1, 1, 0)
-            h_cp(1, 0, 0, S)
-            h_cp(1, 0, 1, S)
-            pe_r(1, 1)
-            hxr(0, 1, G)
-            h_cp(1, 1, 0, S)
-            hxr(1, 1, G)
-            wop(0, 1)
-            pe_da(0, 1, 0)
-            drop(0, 1, 0)
-            pe_da(1, 0, 0)
-            q_w("h", 1, 0)
-            pe_da(0, 1, 1)
-            drop(0, 1, 1)
-            x_il(0, 1, S)
-            pe_r(0, 2)
-            x_il(0, 0, S)
-            wop(1, 1)
-            qdr(0)
-            pe_h(1, 1, 1)
-            pe_da(1, 0, 1)
-            o_mm("h", 0, 1)
-            h_cp(1, 1, 1, S)
-            drop(1, 0, 0)
-            hxr(0, 2, G)
-            drop(1, 0, 1)
-            o_mm("h", 0, 0)
-            pe_da(1, 1, 0)
-            pe_da(1, 1, 1)
-            pe_da(2, 0, 0)
-            widen(1, 1, V)
-            q_w("h", 1, 1)
-            o_mm("h", 0, 2)
-            drop(1, 1, 0)
-            drop(1, 1, 1)
-            pe_r(1, 2)
-            o_cp("h", 0, 1, S)
-            q_w("x", 0, 1)
-            o_cp("h", 0, 0, S)
-            qdr(1)
-            o_cp("h", 0, 2, V)
+            il_cp("h", 1, 1, 1, S)
+            pe_da(0, 0, 1)
+            il_cp("h", 1, 1, 0, S)
+            wop(1, 0)
+            qe(3)
+            pe_il("x", 0, 0, 1)
+            pe_il("x", 0, 1, 1)
+            il_cp("h", 0, 1, 0, S)
             widen(1, 0, S)
-            wop(0, 2)
-            pe_da(2, 0, 1)
-            q_w("x", 0, 0)
-            o_mm("h", 1, 0)
-            x_il(1, 0, S)
-            o_st("h", 0, 0)
+            drop(0, 0, 1)
+            pe_da(0, 1, 1)
+            widen(1, 2, S)
+            pe_il("h", 1, 0, 1)
+            il_cp("h", 1, 0, 1, S)
+            t1(1, 1)
+            pe_da(0, 1, 0)
+            drop(0, 0, 0)
+            widen(1, 1, S)
+            drop(0, 1, 1)
+            pe_da(1, 1, 0)
+            pe_da(1, 0, 0)
+            pe_il("x", 0, 1, 0)
+            pe_da(1, 0, 1)
+            il_cp("x", 0, 1, 1, S)
+            drop(0, 1, 0)
+            q_w("h", 1, 1)
+            il_cp("x", 0, 0, 1, S)
+            il_cp("x", 0, 1, 0, S)
+            qdr(0)
+            q_w("h", 1, 0)
+            q_w("h", 0, 1)
+            widen(1, 3, S)
+            pe_da(1, 1, 1)
+            o_mm("h", 0, 0)
+            wop(1, 1)
+            o_mm("h", 0, 1)
             o_mm("h", 0, 3)
-            o_cp("h", 1, 0, S)
+            o_cp("h", 0, 0, S)
+            q_w("x", 0, 1)
+            wop(0, 1)
+            o_cp("h", 0, 1, S)
+            pe_il("x", 1, 1, 1)
+            pe_il("x", 0, 0, 0)
             o_cp("h", 0, 3, S)
-            pe_da(2, 1, 0)
-            q_w("x", 1, 0)
-            o_mm("h", 1, 2)
-            o_mm("h", 1, 1)
-            o_cp("h", 1, 1, S)
-            drop(2, 0, 0)
-            x_il(1, 1, V)
-            o_cp("h", 1, 2, S)
-            o_mm("h", 1, 3)
+            il_cp("x", 0, 0, 0, S)
+            drop(1, 1, 1)
+            drop(1, 0, 0)
+            drop(1, 1, 0)
+            o_mm("h", 0, 2)
+            drop(1, 0, 1)
+            pe_il("x", 1, 0, 0)
+            q_w("x", 0, 0)
+            il_cp("x", 1, 1, 1, S)
+            pe_il("x", 1, 0, 1)
+            o_cp("h", 0, 2, S)
+            il_cp("x", 1, 0, 1, S)
+            pe_da(2, 0, 1)
             pe_da(2, 1, 1)
-            q_w("x", 1, 1)
-            pe_r(0, 3)
-            o_mm("x", 0, 0)
-            hxr(1, 2, G)
+            qdr(1)
+            o_mm("h", 1, 1)
+            pe_da(2, 1, 0)
+            o_mm("h", 1, 0)
+            o_st("h", 0, 0)
+            il_cp("x", 1, 0, 0, S)
+            pe_il("x", 1, 1, 0)
+            t1(1, 2)
+            t1(0, 2)
+            o_cp("h", 1, 1, S)
+            o_cp("h", 1, 0, S)
+            il_cp("x", 1, 1, 0, S)
+            o_mm("h", 1, 2)
+            q_w("x", 1, 0)
+            wop(0, 2)
+            o_cp("h", 1, 2, S)
             o_st("h", 0, 1)
-            wop(1, 2)
-            o_cp("h", 1, 3, S)
-            o_mm("x", 0, 1)
-            o_st("h", 1, 0)
-            drop(2, 0, 1)
-            o_cp("x", 0, 0, S)
-            drop(2, 1, 1)
-            o_mm("x", 0, 3)
-            o_cp("x", 0, 1, S)
-            o_cp("x", 0, 3, S)
-            o_st("h", 1, 1)
-            o_mm("x", 0, 2)
-            hxr(0, 3, G)
-            drop(2, 1, 0)
-            o_cp("x", 0, 2, S)
-            o_st("x", 0, 0)
-            qdr(2)
-            o_mm("x", 1, 1)
-            pe_da(3, 0, 0)
-            o_mm("x", 1, 2)
+            o_mm("h", 1, 3)
             o_mm("x", 1, 0)
+            q_w("x", 1, 1)
+            o_cp("h", 1, 3, S)
+            pe_da(2, 0, 0)
+            o_cp("x", 1, 0, S)
+            drop(2, 0, 1)
+            o_mm("x", 1, 1)
+            wop(1, 2)
+            o_mm("x", 0, 0)
+            pe_da(3, 0, 0)
+            o_mm("x", 0, 1)
             o_cp("x", 1, 1, S)
-            o_cp("x", 1, 0, V)
-            o_cp("x", 1, 2, S)
-            o_mm("x", 1, 3)
-            o_cp("x", 1, 3, S)
-            pe_r(1, 3)
-            o_mm("h", 2, 1)
-            hxr(1, 3, G)
-            wop(0, 3)
-            o_mm("h", 2, 0)
-            o_cp("h", 2, 0, S)
+            o_mm("x", 0, 3)
+            o_mm("x", 1, 2)
+            o_cp("x", 0, 0, S)
+            o_mm("x", 0, 2)
+            drop(2, 0, 0)
+            drop(2, 1, 1)
+            o_cp("x", 0, 1, S)
+            o_st("h", 1, 0)
+            drop(2, 1, 0)
+            o_cp("x", 0, 3, S)
+            o_cp("x", 0, 2, S)
+            t1(0, 3)
+            o_st("h", 1, 1)
             pe_da(3, 1, 1)
-            o_st("x", 0, 1)
+            o_mm("x", 1, 3)
             o_st("x", 1, 0)
             pe_da(3, 0, 1)
+            qdr(2)
+            t1(1, 3)
+            o_st("x", 0, 0)
+            o_cp("x", 1, 2, S)
+            wop(0, 3)
+            o_cp("x", 1, 3, S)
+            o_mm("h", 2, 0)
+            o_cp("h", 2, 0, S)
+            o_mm("h", 2, 1)
             wop(1, 3)
-            o_cp("h", 2, 1, V)
-            o_st("x", 1, 1)
             o_mm("h", 2, 2)
-            drop(3, 1, 1)
-            o_cp("h", 2, 2, S)
-            o_st("h", 2, 0)
             o_mm("h", 2, 3)
-            o_mm("x", 2, 1)
-            o_cp("h", 2, 3, S)
+            o_st("x", 0, 1)
+            o_cp("h", 2, 1, S)
             drop(3, 0, 0)
-            pe_da(3, 1, 0)
-            drop(3, 0, 1)
-            drop(3, 1, 0)
-            qdr(3)
-            o_cp("x", 2, 1, S)
             o_mm("x", 2, 0)
-            o_mm("x", 2, 3)
-            o_st("h", 2, 1)
-            o_mm("x", 2, 2)
+            o_mm("x", 2, 1)
+            o_st("x", 1, 1)
+            pe_da(3, 1, 0)
+            o_cp("h", 2, 2, S)
+            drop(3, 1, 1)
+            drop(3, 0, 1)
+            o_st("h", 2, 0)
+            o_cp("h", 2, 3, S)
             o_cp("x", 2, 0, S)
-            o_mm("h", 3, 0)
+            o_cp("x", 2, 1, S)
+            drop(3, 1, 0)
+            o_mm("x", 2, 3)
+            o_mm("x", 2, 2)
             o_cp("x", 2, 3, S)
-            o_cp("x", 2, 2, S)
-            o_cp("h", 3, 0, V)
-            o_mm("h", 3, 1)
-            o_mm("h", 3, 3)
-            o_cp("h", 3, 1, V)
-            o_mm("h", 3, 2)
+            o_st("h", 2, 1)
+            qdr(3)
             o_st("x", 2, 0)
-            o_st("x", 2, 1)
-            o_mm("x", 3, 0)
-            o_cp("h", 3, 2, V)
-            o_cp("h", 3, 3, S)
-            o_cp("x", 3, 0, V)
-            o_st("h", 3, 0)
             o_mm("x", 3, 1)
+            o_mm("x", 3, 0)
+            o_cp("x", 2, 2, S)
+            o_mm("h", 3, 0)
+            o_cp("x", 3, 0, V)
+            o_st("x", 2, 1)
+            o_mm("h", 3, 1)
+            o_cp("x", 3, 1, S)
+            o_cp("h", 3, 1, S)
+            o_cp("h", 3, 0, V)
             o_mm("x", 3, 2)
             o_mm("x", 3, 3)
-            o_cp("x", 3, 1, S)
-            o_cp("x", 3, 2, S)
-            o_st("h", 3, 1)
+            o_mm("h", 3, 3)
             o_st("x", 3, 0)
-            o_cp("x", 3, 3, V)
+            o_mm("h", 3, 2)
+            o_cp("x", 3, 2, V)
+            o_cp("x", 3, 3, S)
+            o_st("h", 3, 0)
+            o_cp("h", 3, 2, V)
             o_st("x", 3, 1)
+            o_cp("h", 3, 3, S)
+            o_st("h", 3, 1)

@@ -29,13 +29,11 @@ def tile_gruresetgateweightgradient_w4_kernel(tc, g, z, c, r, h, x_bytes, x_scal
         psum = ctx.enter_context(tc.psum_pool(name="psum", bufs=4))
 
         id_f = keep.tile([P, P], F32, name="id_f")
-        id_b = keep.tile([P, P], BF16, name="id_b")
         ucw = keep.tile([P, 2, 2 * N], U8, align_bytes=64, name="ucw")
         ucs = keep.tile([P, 2, N], U8, align_bytes=64, name="ucs")
         xs = keep.tile([P, 2, 4], F32, name="xs")
         zero = keep.tile([P, 1], F32, name="zero")
         make_identity(nc, id_f[:])
-        make_identity(nc, id_b[:])
 
         def rows(ap):
             return ap.rearrange("(g p t) i -> g p t i", g=2, p=P, t=4)
@@ -49,7 +47,7 @@ def tile_gruresetgateweightgradient_w4_kernel(tc, g, z, c, r, h, x_bytes, x_scal
             d, src = {"z": (zt, gz), "g": (gt, gg), "c": (ct, gc)}[nm]
             gi, tp = divmod(pi, 2)
             if pi not in d:
-                d[pi] = pool.tile([P, 2, N], BF16, tag="ld", bufs=8, name=nm + str(pi))
+                d[pi] = pool.tile([P, 2, N], BF16, tag="ld", bufs=13, name=nm + str(pi))
             lo, hi = (0, 2) if t is None else (t, t + 1)
             nc.sync.dma_start(out=d[pi][:, lo:hi, :], in_=src[gi][:, 2 * tp + lo : 2 * tp + hi, :])
 
@@ -82,7 +80,7 @@ def tile_gruresetgateweightgradient_w4_kernel(tc, g, z, c, r, h, x_bytes, x_scal
             nc.scalar.activation(out=c2[pi, t][:], in_=ct[pi][:, t, :], func=ACT.Square)
 
         def s1(pi, t):
-            av[pi, t] = pool.tile([P, N], F32, tag="av", bufs=3, name="a_%d%d" % (pi, t))
+            av[pi, t] = pool.tile([P, N], F32, tag="av", bufs=6, name="a_%d%d" % (pi, t))
             nc.vector.scalar_tensor_tensor(out=av[pi, t][:], in0=zt[pi][:, t, :], scalar=1.0, in1=gt[pi][:, t, :], op0=ALU.subtract, op1=ALU.mult)
 
         def s2(pi, t):
@@ -107,25 +105,14 @@ def tile_gruresetgateweightgradient_w4_kernel(tc, g, z, c, r, h, x_bytes, x_scal
             es[pi] = keep.tile([P, 512], U8, align_bytes=64, name="es_%d" % pi)
             nc.vector.quantize_mx(out=ec[pi][:].bitcast(FP8X4), scales=es[pi][:], in_=eg[pi][:])
 
-        il = {}
-
-        def pe_il(nm, gi, half, j):
-            bank = psum.tile([P, 2 * 512], BF16, tag="mm", bufs=4, name="il_%s%d%d%d" % (nm, gi, half, j))
-            il[nm, gi, half, j] = bank
-            for k in range(2):
-                c0 = 512 * half + 256 * j + 128 * k
-                nc.tensor.matmul(
-                    bank[:, 512 * k : 512 * (k + 1)].rearrange("p (n t) -> p n t", t=4),
-                    lhsT=id_b[:],
-                    rhs=quad[nm, gi][:, :, c0 : c0 + 128].rearrange("p t n -> p n t"),
-                    start=True, stop=True)
-
         ht = {}
 
         def il_cp(nm, gi, half, j, eng):
             if (nm, gi, half) not in ht:
                 ht[nm, gi, half] = pool.tile([P, 512, 4], BF16, tag="il" + nm, bufs=2 if nm == "x" else 4, align_bytes=64, name="ilt_%s%d%d" % (nm, gi, half))
-            copy(eng, ht[nm, gi, half][:, 256 * j : 256 * (j + 1), :].rearrange("p n t -> p (n t)"), il[nm, gi, half, j][:])
+            c0 = 512 * half + 256 * j
+            dst = ht[nm, gi, half][:, 256 * j : 256 * (j + 1), :].rearrange("p (c i) t -> p c t i", i=4)
+            copy(eng, dst, quad[nm, gi][:, :, c0 : c0 + 256].rearrange("p t (c i) -> p c t i", i=4))
 
         qc, qs = {}, {}
 
@@ -154,7 +141,7 @@ def tile_gruresetgateweightgradient_w4_kernel(tc, g, z, c, r, h, x_bytes, x_scal
         w = {}
 
         def t1(gi, b):
-            w[gi, b] = pool.tile([P, CH, 4], F32, tag="w", bufs=4, name="w_%d%d" % (gi, b))
+            w[gi, b] = pool.tile([P, CH, 4], F32, tag="av", bufs=6, name="w_%d%d" % (gi, b))
             rr = quad["r", gi][:, :, CH * b : CH * (b + 1)].rearrange("p t n -> p n t")
             nc.vector.scalar_tensor_tensor(out=w[gi, b][:], in0=rr, scalar=1.0, in1=rr, op0=ALU.subtract, op1=ALU.mult)
 
@@ -207,267 +194,254 @@ def tile_gruresetgateweightgradient_w4_kernel(tc, g, z, c, r, h, x_bytes, x_scal
                         start=(gi == 0), stop=(gi == 1))
 
         def o_cp(nm, b, q, eng):
-            if (nm, b, q // 2) not in res:
-                res[nm, b, q // 2] = pool.tile([P, 4, CH], F32, tag="out", bufs=4, name="r_%s%d%d" % (nm, b, q // 2))
-            copy(eng, res[nm, b, q // 2][:, 2 * (q % 2) : 2 * (q % 2) + 2, :], obank[nm, b, q][:])
+            fine = b == N // CH - 1
+            key = (nm, b, q if fine else q // 2)
+            m0 = 0 if fine else 2 * (q % 2)
+            if key not in res:
+                res[key] = pool.tile([P, 2 if fine else 4, CH], F32, tag="ld", bufs=13, name="r_%s%d%d" % key)
+            copy(eng, res[key][:, m0 : m0 + 2, :], obank[nm, b, q][:])
 
-        def o_st(nm, b, q2):
+        def o_st(nm, b, s):
             dst = out_0 if nm == "h" else out_1
-            r0 = 512 * q2
-            nc.sync.dma_start(out=dst[r0 : r0 + 512, CH * b : CH * (b + 1)].rearrange("(m p) i -> p m i", p=P), in_=res[nm, b, q2][:])
+            nrow = 256 if b == N // CH - 1 else 512
+            nc.sync.dma_start(out=dst[nrow * s : nrow * (s + 1), CH * b : CH * (b + 1)].rearrange("(m p) i -> p m i", p=P), in_=res[nm, b, s][:])
 
         nc.gpsimd.memset(zero[:], 0.0)
         nc.gpsimd.memset(ucs[:].rearrange("p k n -> p (k n)").bitcast(U32), 0)
         with tc.manual_schedule():
             nc.scalar.activation(out=zero[:], in_=zero[:], func=ACT.Square)
             load_zgc("z", 0, 1)
-            load_zgc("z", 0, 0)
-            load_zgc("g", 0, 1)
             load_zgc("c", 0, 1)
-            s1(0, 1)
-            sq(0, 1)
+            load_zgc("g", 0, 1)
             load_zgc("g", 0, 0)
+            load_zgc("z", 0, 0)
             load_zgc("c", 0, 0)
-            load_zgc("z", 1, None)
-            s1(0, 0)
-            s2(0, 1)
-            tr(0, 1)
-            sq(0, 0)
-            s2(0, 0)
             load_zgc("g", 1, None)
+            load_zgc("z", 1, None)
             load_zgc("c", 1, None)
             load_zgc("g", 2, None)
-            tcp(0, 1, S)
-            s1(1, 0)
-            tr(0, 0)
-            sq(1, 0)
+            sq(0, 1)
             load_zgc("z", 2, None)
-            s1(1, 1)
+            s1(0, 1)
             load_zgc("c", 3, None)
-            s2(1, 0)
-            load_zgc("c", 2, None)
-            s1(2, 0)
-            load_zgc("z", 3, None)
-            sq(1, 1)
-            tr(1, 0)
             load_zgc("g", 3, None)
-            load_quad("h", 0)
-            pe_il("h", 0, 1, 1)
+            s1(0, 0)
+            load_zgc("z", 3, None)
+            sq(0, 0)
+            load_zgc("c", 2, None)
+            s2(0, 1)
             load_xs()
-            load_us(0)
-            load_us(1)
-            load_us(2)
-            load_us(3)
-            load_uw()
-            load_quad("r", 0)
-            s1(2, 1)
-            sq(2, 1)
-            sq(2, 0)
-            s2(1, 1)
-            tcp(1, 0, S)
-            pe_il("h", 0, 0, 1)
-            s2(2, 1)
-            tcp(0, 0, S)
             load_x(0)
-            pe_il("h", 0, 0, 0)
-            load_quad("h", 1)
-            sq(3, 0)
-            s1(3, 0)
-            tr(1, 1)
-            s2(2, 0)
-            sq(3, 1)
-            s1(3, 1)
-            il_cp("h", 0, 0, 1, S)
-            tcp(1, 1, S)
-            il_cp("h", 0, 0, 0, S)
-            qe(0)
-            il_cp("h", 0, 1, 1, S)
-            s2(3, 0)
+            s2(0, 0)
+            tr(0, 1)
+            load_x(1)
+            tcp(0, 1, S)
+            s1(1, 1)
+            tr(0, 0)
+            sq(1, 1)
+            load_quad("r", 0)
+            s1(1, 0)
+            tcp(0, 0, S)
             load_quad("r", 1)
+            s2(1, 1)
+            sq(1, 0)
+            qe(0)
+            load_quad("h", 1)
+            tr(1, 1)
+            s2(1, 0)
+            tcp(1, 1, S)
+            load_us(0), load_us(1), load_us(2), load_us(3), load_uw()
+            sq(3, 0)
+            s1(2, 0)
+            tr(1, 0)
+            load_quad("h", 0)
+            tcp(1, 0, S)
+            s1(2, 1)
+            sq(3, 1)
+            s1(3, 0)
+            sq(2, 0)
+            qe(1)
+            s1(3, 1)
             widen(0, 2, S)
+            s2(2, 0)
+            widen(0, 1, S)
+            s2(3, 1)
+            tr(2, 0)
+            widen(0, 3, S)
+            s2(3, 0)
+            tr(3, 1)
+            tcp(2, 0, S)
+            widen(0, 0, S)
             t1(0, 0)
             tr(3, 0)
-            qe(1)
-            tcp(3, 0, S)
-            q_w("h", 0, 0)
-            widen(0, 3, S)
-            tr(2, 0)
-            s2(3, 1)
-            pe_il("h", 1, 0, 0)
-            widen(0, 0, S)
-            tcp(2, 0, S)
-            tr(2, 1)
-            tr(3, 1)
-            il_cp("h", 1, 0, 0, S)
-            tcp(2, 1, S)
-            wop(0, 0)
-            pe_il("h", 1, 1, 1)
-            load_x(1)
-            t1(0, 1)
-            widen(0, 1, S)
-            t1(1, 0)
             tcp(3, 1, S)
-            pe_il("h", 0, 1, 0)
-            pe_il("h", 1, 1, 0)
-            qe(2)
-            pe_da(0, 0, 0)
-            il_cp("h", 1, 1, 1, S)
-            pe_da(0, 0, 1)
+            t1(0, 1)
+            sq(2, 1)
+            t1(1, 2)
+            tcp(3, 0, S)
+            il_cp("x", 0, 0, 0, S)
+            s2(2, 1)
             il_cp("h", 1, 1, 0, S)
-            wop(1, 0)
+            t1(1, 1)
+            tr(2, 1)
+            il_cp("h", 1, 1, 1, S)
+            t1(1, 0)
+            pe_da(1, 0, 1)
+            tcp(2, 1, S)
+            pe_da(0, 0, 0)
             qe(3)
-            pe_il("x", 0, 0, 1)
-            pe_il("x", 0, 1, 1)
-            il_cp("h", 0, 1, 0, S)
+            il_cp("h", 1, 0, 1, S)
+            pe_da(1, 0, 0)
+            qe(2)
+            pe_da(0, 0, 1)
+            q_w("h", 1, 1)
+            il_cp("h", 0, 0, 1, S)
+            wop(1, 1)
+            il_cp("h", 0, 0, 0, S)
+            wop(0, 1)
+            il_cp("h", 0, 1, 1, S)
+            wop(0, 0)
+            il_cp("h", 1, 0, 0, S)
+            drop(1, 0, 1)
+            drop(0, 0, 0)
+            pe_da(1, 1, 1)
             widen(1, 0, S)
             drop(0, 0, 1)
-            pe_da(0, 1, 1)
-            widen(1, 2, S)
-            pe_il("h", 1, 0, 1)
-            il_cp("h", 1, 0, 1, S)
-            t1(1, 1)
-            pe_da(0, 1, 0)
-            drop(0, 0, 0)
-            widen(1, 1, S)
-            drop(0, 1, 1)
             pe_da(1, 1, 0)
-            pe_da(1, 0, 0)
-            pe_il("x", 0, 1, 0)
-            pe_da(1, 0, 1)
-            il_cp("x", 0, 1, 1, S)
-            drop(0, 1, 0)
-            q_w("h", 1, 1)
-            il_cp("x", 0, 0, 1, S)
-            il_cp("x", 0, 1, 0, S)
-            qdr(0)
-            q_w("h", 1, 0)
-            q_w("h", 0, 1)
-            widen(1, 3, S)
-            pe_da(1, 1, 1)
-            o_mm("h", 0, 0)
-            wop(1, 1)
-            o_mm("h", 0, 1)
-            o_mm("h", 0, 3)
-            o_cp("h", 0, 0, S)
-            q_w("x", 0, 1)
-            wop(0, 1)
-            o_cp("h", 0, 1, S)
-            pe_il("x", 1, 1, 1)
-            pe_il("x", 0, 0, 0)
-            o_cp("h", 0, 3, S)
-            il_cp("x", 0, 0, 0, S)
             drop(1, 1, 1)
-            drop(1, 0, 0)
+            widen(1, 2, S)
             drop(1, 1, 0)
-            o_mm("h", 0, 2)
-            drop(1, 0, 1)
-            pe_il("x", 1, 0, 0)
-            q_w("x", 0, 0)
-            il_cp("x", 1, 1, 1, S)
-            pe_il("x", 1, 0, 1)
-            o_cp("h", 0, 2, S)
-            il_cp("x", 1, 0, 1, S)
-            pe_da(2, 0, 1)
-            pe_da(2, 1, 1)
+            drop(1, 0, 0)
+            widen(1, 3, S)
+            wop(1, 0)
+            pe_da(0, 1, 1)
+            pe_da(0, 1, 0)
+            widen(1, 1, S)
             qdr(1)
-            o_mm("h", 1, 1)
+            pe_da(2, 0, 1)
+            drop(0, 1, 0)
             pe_da(2, 1, 0)
-            o_mm("h", 1, 0)
-            o_st("h", 0, 0)
+            il_cp("h", 0, 1, 0, S)
+            drop(0, 1, 1)
+            q_w("h", 0, 0)
+            pe_da(2, 1, 1)
+            il_cp("x", 0, 0, 1, S)
+            qdr(0)
+            pe_da(3, 1, 0)
+            q_w("h", 0, 1)
             il_cp("x", 1, 0, 0, S)
-            pe_il("x", 1, 1, 0)
-            t1(1, 2)
             t1(0, 2)
-            o_cp("h", 1, 1, S)
-            o_cp("h", 1, 0, S)
-            il_cp("x", 1, 1, 0, S)
             o_mm("h", 1, 2)
-            q_w("x", 1, 0)
-            wop(0, 2)
-            o_cp("h", 1, 2, S)
-            o_st("h", 0, 1)
             o_mm("h", 1, 3)
-            o_mm("x", 1, 0)
-            q_w("x", 1, 1)
+            o_cp("h", 1, 2, S)
+            q_w("x", 0, 0)
+            o_mm("h", 0, 3)
             o_cp("h", 1, 3, S)
-            pe_da(2, 0, 0)
-            o_cp("x", 1, 0, S)
+            o_mm("h", 0, 2)
+            wop(0, 2)
+            o_cp("h", 0, 3, S)
+            o_st("h", 1, 1)
+            o_cp("h", 0, 2, S)
+            q_w("h", 1, 0)
+            il_cp("x", 1, 1, 0, S)
+            o_st("h", 0, 1)
             drop(2, 0, 1)
-            o_mm("x", 1, 1)
+            o_mm("h", 0, 0)
             wop(1, 2)
-            o_mm("x", 0, 0)
-            pe_da(3, 0, 0)
+            o_mm("h", 1, 1)
+            il_cp("x", 1, 0, 1, S)
+            o_mm("h", 0, 1)
+            o_cp("h", 0, 0, V)
+            o_mm("h", 1, 0)
+            drop(2, 1, 0)
+            o_cp("h", 0, 1, S)
+            pe_da(3, 1, 1)
+            q_w("x", 1, 0)
+            o_cp("h", 1, 1, S)
+            o_st("h", 0, 0)
+            pe_da(2, 0, 0)
+            il_cp("x", 1, 1, 1, S)
+            o_cp("h", 1, 0, V)
             o_mm("x", 0, 1)
-            o_cp("x", 1, 1, S)
-            o_mm("x", 0, 3)
-            o_mm("x", 1, 2)
-            o_cp("x", 0, 0, S)
-            o_mm("x", 0, 2)
             drop(2, 0, 0)
+            o_st("h", 1, 0)
+            o_mm("x", 0, 0)
             drop(2, 1, 1)
             o_cp("x", 0, 1, S)
-            o_st("h", 1, 0)
-            drop(2, 1, 0)
-            o_cp("x", 0, 3, S)
-            o_cp("x", 0, 2, S)
-            t1(0, 3)
-            o_st("h", 1, 1)
-            pe_da(3, 1, 1)
-            o_mm("x", 1, 3)
-            o_st("x", 1, 0)
-            pe_da(3, 0, 1)
+            o_mm("x", 1, 0)
+            q_w("x", 1, 1)
+            o_cp("x", 0, 0, S)
+            o_mm("x", 1, 1)
             qdr(2)
-            t1(1, 3)
+            o_cp("x", 1, 0, S)
+            pe_da(3, 0, 0)
             o_st("x", 0, 0)
-            o_cp("x", 1, 2, S)
-            wop(0, 3)
-            o_cp("x", 1, 3, S)
-            o_mm("h", 2, 0)
-            o_cp("h", 2, 0, S)
+            o_cp("x", 1, 1, S)
+            il_cp("x", 0, 1, 0, V)
             o_mm("h", 2, 1)
-            wop(1, 3)
-            o_mm("h", 2, 2)
-            o_mm("h", 2, 3)
-            o_st("x", 0, 1)
+            il_cp("x", 0, 1, 1, V)
+            o_st("x", 1, 0)
+            o_mm("h", 2, 0)
             o_cp("h", 2, 1, S)
-            drop(3, 0, 0)
-            o_mm("x", 2, 0)
+            o_mm("h", 2, 3)
+            t1(1, 3)
+            o_cp("h", 2, 0, S)
             o_mm("x", 2, 1)
-            o_st("x", 1, 1)
-            pe_da(3, 1, 0)
-            o_cp("h", 2, 2, S)
-            drop(3, 1, 1)
-            drop(3, 0, 1)
-            o_st("h", 2, 0)
             o_cp("h", 2, 3, S)
-            o_cp("x", 2, 0, S)
+            o_st("h", 2, 0)
+            o_mm("h", 2, 2)
+            q_w("x", 0, 1)
             o_cp("x", 2, 1, S)
-            drop(3, 1, 0)
-            o_mm("x", 2, 3)
-            o_mm("x", 2, 2)
-            o_cp("x", 2, 3, S)
+            o_mm("x", 2, 0)
+            wop(1, 3)
+            o_cp("h", 2, 2, S)
+            o_mm("x", 1, 3)
+            o_cp("x", 2, 0, S)
             o_st("h", 2, 1)
-            qdr(3)
+            o_mm("x", 1, 2)
+            t1(0, 3)
+            o_cp("x", 1, 3, S)
             o_st("x", 2, 0)
-            o_mm("x", 3, 1)
-            o_mm("x", 3, 0)
+            o_mm("x", 0, 2)
+            o_cp("x", 1, 2, S)
+            o_mm("x", 2, 3)
+            o_cp("x", 0, 2, S)
+            drop(3, 1, 0)
+            o_mm("x", 0, 3)
+            o_st("x", 1, 1)
+            o_cp("x", 2, 3, S)
+            wop(0, 3)
+            o_mm("x", 2, 2)
+            o_cp("x", 0, 3, S)
+            pe_da(3, 0, 1)
             o_cp("x", 2, 2, S)
-            o_mm("h", 3, 0)
-            o_cp("x", 3, 0, V)
+            drop(3, 1, 1)
+            o_st("x", 0, 1)
+            drop(3, 0, 0)
             o_st("x", 2, 1)
-            o_mm("h", 3, 1)
-            o_cp("x", 3, 1, S)
-            o_cp("h", 3, 1, S)
-            o_cp("h", 3, 0, V)
-            o_mm("x", 3, 2)
-            o_mm("x", 3, 3)
-            o_mm("h", 3, 3)
-            o_st("x", 3, 0)
+            drop(3, 0, 1)
+            qdr(3)
             o_mm("h", 3, 2)
+            o_mm("x", 3, 2)
+            o_cp("h", 3, 2, S)
+            o_mm("h", 3, 3)
             o_cp("x", 3, 2, V)
-            o_cp("x", 3, 3, S)
+            o_st("h", 3, 2)
+            o_mm("h", 3, 0)
+            o_cp("h", 3, 3, V)
+            o_st("h", 3, 3)
+            o_mm("h", 3, 1)
+            o_cp("h", 3, 0, V)
+            o_mm("x", 3, 1)
             o_st("h", 3, 0)
-            o_cp("h", 3, 2, V)
-            o_st("x", 3, 1)
-            o_cp("h", 3, 3, S)
+            o_cp("h", 3, 1, S)
+            o_mm("x", 3, 0)
             o_st("h", 3, 1)
+            o_cp("x", 3, 1, V)
+            o_st("x", 3, 1)
+            o_mm("x", 3, 3)
+            o_cp("x", 3, 0, V)
+            o_st("x", 3, 0)
+            o_cp("x", 3, 3, S)
+            o_st("x", 3, 3)
+            o_st("x", 3, 2)

@@ -17,8 +17,10 @@ ACT = mybir.ActivationFunctionType
 P = 128
 N = 1024
 FLOPS = 3 * 2 * N * N * N
-CH = 256
-V, S, G = "v", "s", "g"
+CW = [256, 256, 256, 128, 128]
+HW = [256, 256, 256, 256]
+XW = [256, 256, 256, 128, 128]
+V, S = "v", "s"
 
 
 def tile_gruresetgateweightgradient_w4_kernel(tc, g, z, c, r, h, x_bytes, x_scale, uc_words, uc_scales, out_0, out_1):
@@ -43,13 +45,14 @@ def tile_gruresetgateweightgradient_w4_kernel(tc, g, z, c, r, h, x_bytes, x_scal
 
         zt, gt, ct = {}, {}, {}
 
-        def load_zgc(nm, pi, t):
+        def load_zgc(nm, pi, t, half=None):
             d, src = {"z": (zt, gz), "g": (gt, gg), "c": (ct, gc)}[nm]
             gi, tp = divmod(pi, 2)
             if pi not in d:
                 d[pi] = pool.tile([P, 2, N], BF16, tag="ld", bufs=13, name=nm + str(pi))
             lo, hi = (0, 2) if t is None else (t, t + 1)
-            nc.sync.dma_start(out=d[pi][:, lo:hi, :], in_=src[gi][:, 2 * tp + lo : 2 * tp + hi, :])
+            cols = slice(0, N) if half is None else slice(512 * half, 512 * (half + 1))
+            nc.sync.dma_start(out=d[pi][:, lo:hi, cols], in_=src[gi][:, 2 * tp + lo : 2 * tp + hi, cols])
 
         def load_uw():
             nc.sync.dma_start(out=ucw[:], in_=uc_words.rearrange("k p n -> p k n"))
@@ -64,7 +67,7 @@ def tile_gruresetgateweightgradient_w4_kernel(tc, g, z, c, r, h, x_bytes, x_scal
 
         def load_quad(nm, gi):
             src = gh if nm == "h" else gr
-            quad[nm, gi] = pool.tile([P, 4, N], BF16, tag="q4" if nm == "h" else "r4", bufs=3 if nm == "h" else 2, name=nm + str(gi))
+            quad[nm, gi] = pool.tile([P, 4, N], BF16, tag=nm + "4", bufs=2, name=nm + str(gi))
             nc.sync.dma_start(out=quad[nm, gi][:], in_=src[gi])
 
         def copy(eng, out, in_):
@@ -73,55 +76,47 @@ def tile_gruresetgateweightgradient_w4_kernel(tc, g, z, c, r, h, x_bytes, x_scal
             else:
                 nc.scalar.copy(out=out, in_=in_)
 
-        c2, av, eb, xt, eg, ec, es = {}, {}, {}, {}, {}, {}, {}
+        cb, c2, av, ab, eg, ec, es = {}, {}, {}, {}, {}, {}, {}
 
-        def sq(pi, t):
-            c2[pi, t] = pool.tile([P, N], F32, tag="c2", bufs=3, name="c2_%d%d" % (pi, t))
-            nc.scalar.activation(out=c2[pi, t][:], in_=ct[pi][:, t, :], func=ACT.Square)
-
-        def s1(pi, t):
-            av[pi, t] = pool.tile([P, N], F32, tag="av", bufs=6, name="a_%d%d" % (pi, t))
-            nc.vector.scalar_tensor_tensor(out=av[pi, t][:], in0=zt[pi][:, t, :], scalar=1.0, in1=gt[pi][:, t, :], op0=ALU.subtract, op1=ALU.mult)
-
-        def s2(pi, t):
-            eb[pi, t] = pool.tile([P, N], BF16, tag="eb", bufs=4, align_bytes=64, name="e_%d%d" % (pi, t))
-            nc.vector.scalar_tensor_tensor(out=eb[pi, t][:], in0=c2[pi, t][:], scalar=1.0, in1=av[pi, t][:], op0=ALU.subtract, op1=ALU.mult)
-
-        def tr(pi, t):
-            xt[pi, t] = psum.tile([P, 2, 2, P], F32, tag="mm", bufs=4, name="xt_%d%d" % (pi, t))
-            words = eb[pi, t][:].bitcast(F32)
+        def trc(pi, t):
+            cb[pi, t] = psum.tile([P, 2, 2, P], F32, tag="mm", bufs=5, name="cb_%d%d" % (pi, t))
+            words = ct[pi][:, t, :].bitcast(F32)
             for k in range(2):
                 for u in range(2):
-                    nc.tensor.transpose(xt[pi, t][:, k, u, :], words[:, 256 * k + u : 256 * (k + 1) : 2], id_f[:])
+                    nc.tensor.transpose(cb[pi, t][:, u, k, :], words[:, 256 * k + u : 256 * (k + 1) : 2], id_f[:])
 
-        def tcp(pi, t, eng):
+        def sq(pi, t):
+            c2[pi, t] = pool.tile([P, 2, P, 4], F32, tag="c2", bufs=3, name="c2_%d%d" % (pi, t))
+            src = cb[pi, t][:].rearrange("p u k n -> p (u k n)").bitcast(BF16).rearrange("p (u m e) -> p m u e", u=2, e=2)
+            dst = c2[pi, t][:].rearrange("p k n (u e) -> p (k n) u e", e=2)
+            nc.scalar.activation(out=dst, in_=src, func=ACT.Square)
+
+        def s1(pi, t, k=None):
+            if (pi, t) not in av:
+                av[pi, t] = pool.tile([P, 4, 2 * P], F32, tag="av", bufs=6, name="a_%d%d" % (pi, t))
+            js = slice(0, 2 * P) if k is None else slice(P * k, P * (k + 1))
+
+            def by_u(tile):
+                return tile[:, t, :].rearrange("p (j u) -> p u j", u=4)[:, :, js]
+
+            nc.vector.scalar_tensor_tensor(out=av[pi, t][:, :, js], in0=by_u(zt[pi]), scalar=1.0, in1=by_u(gt[pi]), op0=ALU.subtract, op1=ALU.mult)
+
+        def tra(pi, t, k):
+            ab[pi, t, k] = psum.tile([P, 4, P], F32, tag="da", bufs=3, name="ab_%d%d%d" % (pi, t, k))
+            for u in range(4):
+                nc.tensor.transpose(ab[pi, t, k][:, u, :], av[pi, t][:, u, P * k : P * (k + 1)], id_f[:])
+
+        def s2(pi, t, k):
             if pi not in eg:
-                eg[pi] = pool.tile([P, 2 * 2 * P * 4], BF16, tag="eg", bufs=2, align_bytes=64, name="eg_%d" % pi)
-            dst = eg[pi][:].bitcast(F32)[:, 512 * t : 512 * (t + 1)].rearrange("p (k m u) -> p k m u", k=2, u=2)
-            copy(eng, dst, xt[pi, t][:].rearrange("p k u m -> p k m u"))
+                eg[pi] = pool.tile([P, 2, 2, P, 4], BF16, tag="eg", bufs=2, align_bytes=64, name="eg_%d" % pi)
+            nc.vector.scalar_tensor_tensor(
+                out=eg[pi][:, t, k], in0=c2[pi, t][:, k], scalar=1.0, in1=ab[pi, t, k][:].rearrange("p u n -> p n u"),
+                op0=ALU.subtract, op1=ALU.mult)
 
         def qe(pi):
             ec[pi] = keep.tile([P, 512], U32, align_bytes=64, name="ec_%d" % pi)
             es[pi] = keep.tile([P, 512], U8, align_bytes=64, name="es_%d" % pi)
-            nc.vector.quantize_mx(out=ec[pi][:].bitcast(FP8X4), scales=es[pi][:], in_=eg[pi][:])
-
-        ht = {}
-
-        def il_cp(nm, gi, half, j, eng):
-            if (nm, gi, half) not in ht:
-                ht[nm, gi, half] = pool.tile([P, 512, 4], BF16, tag="il" + nm, bufs=2 if nm == "x" else 4, align_bytes=64, name="ilt_%s%d%d" % (nm, gi, half))
-            c0 = 512 * half + 256 * j
-            dst = ht[nm, gi, half][:, 256 * j : 256 * (j + 1), :].rearrange("p (c i) t -> p c t i", i=4)
-            copy(eng, dst, quad[nm, gi][:, :, c0 : c0 + 256].rearrange("p t (c i) -> p c t i", i=4))
-
-        qc, qs = {}, {}
-
-        def q_w(nm, gi, half):
-            if (nm, gi) not in qc:
-                qc[nm, gi] = keep.tile([P, N], U32, align_bytes=64, name="qc_%s%d" % (nm, gi))
-                qs[nm, gi] = keep.tile([P, N], U8, align_bytes=64, name="qs_%s%d" % (nm, gi))
-            sl = slice(512 * half, 512 * (half + 1))
-            nc.vector.quantize_mx(out=qc[nm, gi][:, sl].bitcast(FP8X4), scales=qs[nm, gi][:, sl], in_=ht[nm, gi, half][:].rearrange("p n t -> p (n t)"))
+            nc.vector.quantize_mx(out=ec[pi][:].bitcast(FP8X4), scales=es[pi][:], in_=eg[pi][:].rearrange("p t k n u -> p (t k n u)"))
 
         xb = {}
 
@@ -131,30 +126,56 @@ def tile_gruresetgateweightgradient_w4_kernel(tc, g, z, c, r, h, x_bytes, x_scal
 
         def widen(gi, t, eng):
             if ("x", gi) not in quad:
-                quad["x", gi] = pool.tile([P, 4, N], BF16, tag="q4", bufs=3, name="x" + str(gi))
+                quad["x", gi] = pool.tile([P, 4, N], BF16, tag="x4", bufs=2, name="x" + str(gi))
             src = xb[gi][:, N * t : N * (t + 1)].bitcast(FP8)
             if eng == V:
                 nc.vector.tensor_scalar(out=quad["x", gi][:, t, :], in0=src, scalar1=xs[:, gi, t : t + 1], scalar2=None, op0=ALU.mult)
             else:
                 nc.scalar.activation(out=quad["x", gi][:, t, :], in_=src, func=ACT.Copy, scale=xs[:, gi, t : t + 1])
 
+        il = {}
+        width = {"h": HW, "x": XW, "d": CW}
+
+        def il_cp(nm, gi, b, eng):
+            cw = width[nm][b]
+            if (nm, b) not in il:
+                il[nm, b] = pool.tile([P, 2, cw, 4], BF16, tag="il" + nm, bufs=2 if nm == "x" else 4, align_bytes=64, name="il_%s%d" % (nm, b))
+            c0 = sum(width[nm][:b])
+            dst = il[nm, b][:, gi].rearrange("p (c i) t -> p c t i", i=4)
+            copy(eng, dst, quad[nm, gi][:, :, c0 : c0 + cw].rearrange("p t (c i) -> p c t i", i=4))
+
+        qc, qs = {}, {}
+
+        def quantize(nm, b, src):
+            cw = width[nm][b]
+            qc[nm, b] = keep.tile([P, 2, cw], U32, align_bytes=64, name="qc_%s%d" % (nm, b))
+            qs[nm, b] = keep.tile([P, 2, cw], U8, align_bytes=64, name="qs_%s%d" % (nm, b))
+            nc.vector.quantize_mx(
+                out=qc[nm, b][:].rearrange("p g n -> p (g n)").bitcast(FP8X4), scales=qs[nm, b][:].rearrange("p g n -> p (g n)"),
+                in_=src[:].rearrange("p g n t -> p (g n t)"))
+
+        def q_w(nm, b):
+            quantize(nm, b, il[nm, b])
+
+        def start(nm, b):
+            return sum(width[nm][:b])
+
         w = {}
 
         def t1(gi, b):
-            w[gi, b] = pool.tile([P, CH, 4], F32, tag="av", bufs=6, name="w_%d%d" % (gi, b))
-            rr = quad["r", gi][:, :, CH * b : CH * (b + 1)].rearrange("p t n -> p n t")
+            w[gi, b] = pool.tile([P, 4, CW[b]], F32, tag="av", bufs=6, name="w_%d%d" % (gi, b))
+            rr = quad["r", gi][:, :, start("d", b) : start("d", b + 1)]
             nc.vector.scalar_tensor_tensor(out=w[gi, b][:], in0=rr, scalar=1.0, in1=rr, op0=ALU.subtract, op1=ALU.mult)
 
         def wop(gi, b):
-            o = CH * (b % 2)
-            nc.vector.tensor_tensor(out=w[gi, b][:], in0=w[gi, b][:], in1=ht["h", gi, b // 2][:, o : o + CH, :], op=ALU.mult)
+            nc.vector.tensor_tensor(out=w[gi, b][:], in0=w[gi, b][:], in1=quad["h", gi][:, :, start("d", b) : start("d", b + 1)], op=ALU.mult)
 
         da = {}
 
         def pe_da(b, gi, j):
-            bank = psum.tile([P, 4, P], F32, tag="da", bufs=4, name="da_%d%d%d" % (b, gi, j))
+            bank = psum.tile([P, 4, P], F32, tag="da", bufs=3, name="da_%d%d%d" % (b, gi, j))
             da[b, gi, j] = bank
-            i0 = CH * b + P * j
+            i0 = start("d", b) + P * j
             for t in range(4):
                 pi = 2 * gi + t // 2
                 for k in range(2):
@@ -165,283 +186,312 @@ def tile_gruresetgateweightgradient_w4_kernel(tc, g, z, c, r, h, x_bytes, x_scal
                         rhs=ucw[:, k, 2 * i0 : 2 * (i0 + P)].bitcast(FP4X4), rhs_scale=ucs[:, k, i0 : i0 + P],
                         start=(k == 0), stop=(k == 1))
 
-        dr, dc, ds = {}, {}, {}
+        dr = {}
 
         def drop(b, gi, j):
             if b not in dr:
-                dr[b] = pool.tile([P, 2, CH, 4], BF16, tag="dr", bufs=2, align_bytes=64, name="dr_%d" % b)
-            nc.vector.scalar_tensor_tensor(out=dr[b][:, gi, P * j : P * (j + 1), :], in0=da[b, gi, j][:].rearrange("p t n -> p n t"), scalar=-1.0, in1=w[gi, b][:, P * j : P * (j + 1), :], op0=ALU.mult, op1=ALU.mult)
+                dr[b] = pool.tile([P, 2, CW[b], 4], BF16, tag="dr", bufs=2, align_bytes=64, name="dr_%d" % b)
+            nc.vector.scalar_tensor_tensor(
+                out=dr[b][:, gi, P * j : P * (j + 1), :], in0=da[b, gi, j][:].rearrange("p t n -> p n t"), scalar=-1.0,
+                in1=w[gi, b][:, :, P * j : P * (j + 1)].rearrange("p t n -> p n t"), op0=ALU.mult, op1=ALU.mult)
 
         def qdr(b):
-            dc[b] = keep.tile([P, 2, CH], U32, align_bytes=64, name="dc_%d" % b)
-            ds[b] = keep.tile([P, 2, CH], U8, align_bytes=64, name="ds_%d" % b)
-            nc.vector.quantize_mx(out=dc[b][:].rearrange("p g n -> p (g n)").bitcast(FP8X4), scales=ds[b][:].rearrange("p g n -> p (g n)"), in_=dr[b][:].rearrange("p g n t -> p (g n t)"))
+            quantize("d", b, dr[b])
 
-        res = {}
+        obank, res = {}, {}
 
-        obank = {}
+        def o_mm(nm, ms, bs):
+            bank = psum.tile([P, len(ms), sum(CW[b] for b in bs)], F32, tag="mm", bufs=5, name="o_%s%d_%d" % (nm, ms[0], bs[0]))
+            obank[nm, ms[0], bs[0]] = bank
+            for i, m in enumerate(ms):
+                a = max(k for k in range(len(width[nm])) if start(nm, k) <= P * m)
+                rows_m = slice(P * m - start(nm, a), P * (m + 1) - start(nm, a))
+                c0 = 0
+                for b in bs:
+                    for gi in range(2):
+                        nc.tensor.matmul_mx(
+                            out=bank[:, i, c0 : c0 + CW[b]],
+                            lhsT=qc[nm, a][:, gi, rows_m].bitcast(FP8X4), lhsT_scale=qs[nm, a][:, gi, rows_m],
+                            rhs=qc["d", b][:, gi, :].bitcast(FP8X4), rhs_scale=qs["d", b][:, gi, :],
+                            start=(gi == 0), stop=(gi == 1))
+                    c0 += CW[b]
 
-        def o_mm(nm, b, q):
-            bank = psum.tile([P, 2, CH], F32, tag="mm", bufs=4, name="o_%s%d%d" % (nm, b, q))
-            obank[nm, b, q] = bank
-            for m in range(2):
-                m0 = P * (2 * q + m)
-                for gi in range(2):
-                    nc.tensor.matmul_mx(
-                        out=bank[:, m, :],
-                        lhsT=qc[nm, gi][:, m0 : m0 + P].bitcast(FP8X4), lhsT_scale=qs[nm, gi][:, m0 : m0 + P],
-                        rhs=dc[b][:, gi, :].bitcast(FP8X4), rhs_scale=ds[b][:, gi, :],
-                        start=(gi == 0), stop=(gi == 1))
-
-        def o_cp(nm, b, q, eng):
-            fine = b == N // CH - 1
-            key = (nm, b, q if fine else q // 2)
-            m0 = 0 if fine else 2 * (q % 2)
+        def o_cp(nm, ms, bs, st_ms, st_bs, eng):
+            key = (nm, st_ms[0], st_bs[0])
             if key not in res:
-                res[key] = pool.tile([P, 2 if fine else 4, CH], F32, tag="ld", bufs=13, name="r_%s%d%d" % key)
-            copy(eng, res[key][:, m0 : m0 + 2, :], obank[nm, b, q][:])
+                res[key] = pool.tile([P, len(st_ms), sum(CW[b] for b in st_bs)], F32, tag="ld", bufs=13, name="r_%s%d_%d" % key)
+            i0, c0 = st_ms.index(ms[0]), start("d", bs[0]) - start("d", st_bs[0])
+            copy(eng, res[key][:, i0 : i0 + len(ms), c0 : c0 + sum(CW[b] for b in bs)], obank[nm, ms[0], bs[0]][:])
 
-        def o_st(nm, b, s):
+        def o_st(nm, ms, bs):
             dst = out_0 if nm == "h" else out_1
-            nrow = 256 if b == N // CH - 1 else 512
-            nc.sync.dma_start(out=dst[nrow * s : nrow * (s + 1), CH * b : CH * (b + 1)].rearrange("(m p) i -> p m i", p=P), in_=res[nm, b, s][:])
+            dst = dst[P * ms[0] : P * (ms[-1] + 1), start("d", bs[0]) : start("d", bs[-1] + 1)]
+            nc.sync.dma_start(out=dst.rearrange("(m p) i -> p m i", p=P), in_=res[nm, ms[0], bs[0]][:])
 
         nc.gpsimd.memset(zero[:], 0.0)
         nc.gpsimd.memset(ucs[:].rearrange("p k n -> p (k n)").bitcast(U32), 0)
         with tc.manual_schedule():
             nc.scalar.activation(out=zero[:], in_=zero[:], func=ACT.Square)
+            load_zgc("c", 0, 0)
+            trc(0, 0)
+            sq(0, 0)
+            load_zgc("z", 0, 0, 1)
+            load_zgc("g", 0, 0, 1)
+            s1(0, 0, 1)
+            tra(0, 0, 1)
+            s2(0, 0, 1)
             load_zgc("z", 0, 1)
             load_zgc("c", 0, 1)
             load_zgc("g", 0, 1)
-            load_zgc("g", 0, 0)
-            load_zgc("z", 0, 0)
-            load_zgc("c", 0, 0)
-            load_zgc("g", 1, None)
-            load_zgc("z", 1, None)
-            load_zgc("c", 1, None)
-            load_zgc("g", 2, None)
+            trc(0, 1)
             sq(0, 1)
-            load_zgc("z", 2, None)
             s1(0, 1)
-            load_zgc("c", 3, None)
-            load_zgc("g", 3, None)
-            s1(0, 0)
-            load_zgc("z", 3, None)
-            sq(0, 0)
-            load_zgc("c", 2, None)
-            s2(0, 1)
+            load_zgc("z", 0, 0, 0)
+            load_zgc("g", 0, 0, 0)
+            s1(0, 0, 0)
+            tra(0, 1, 0)
+            s2(0, 1, 0)
+            tra(0, 1, 1)
+            s2(0, 1, 1)
+            tra(0, 0, 0)
+            s2(0, 0, 0)
+            qe(0)
+            load_zgc("c", 1, None)
+            load_zgc("z", 1, None)
+            load_zgc("g", 1, None)
+            trc(1, 1)
+            trc(1, 0)
+            s1(1, 0)
             load_xs()
             load_x(0)
-            s2(0, 0)
-            tr(0, 1)
+            load_zgc("g", 2, None)
+            load_zgc("z", 2, None)
+            load_zgc("c", 2, None)
+            load_zgc("c", 3, None)
             load_x(1)
-            tcp(0, 1, S)
-            s1(1, 1)
-            tr(0, 0)
-            sq(1, 1)
+            load_zgc("g", 3, None)
+            load_zgc("z", 3, None)
             load_quad("r", 0)
-            s1(1, 0)
-            tcp(0, 0, S)
-            load_quad("r", 1)
-            s2(1, 1)
-            sq(1, 0)
-            qe(0)
-            load_quad("h", 1)
-            tr(1, 1)
-            s2(1, 0)
-            tcp(1, 1, S)
-            load_us(0), load_us(1), load_us(2), load_us(3), load_uw()
-            sq(3, 0)
-            s1(2, 0)
-            tr(1, 0)
             load_quad("h", 0)
-            tcp(1, 0, S)
+            load_us(0), load_us(1), load_us(2), load_us(3), load_uw()
+            load_quad("r", 1)
+            load_quad("h", 1)
+            s1(1, 1)
+            sq(1, 1)
+            sq(1, 0)
+            tra(1, 0, 0)
+            tra(1, 0, 1)
+            s2(1, 0, 0)
+            s2(1, 0, 1)
+            tra(1, 1, 0)
+            s2(1, 1, 0)
+            tra(1, 1, 1)
             s1(2, 1)
-            sq(3, 1)
-            s1(3, 0)
-            sq(2, 0)
+            s2(1, 1, 1)
+            s1(2, 0)
             qe(1)
-            s1(3, 1)
             widen(0, 2, S)
-            s2(2, 0)
             widen(0, 1, S)
-            s2(3, 1)
-            tr(2, 0)
-            widen(0, 3, S)
-            s2(3, 0)
-            tr(3, 1)
-            tcp(2, 0, S)
             widen(0, 0, S)
-            t1(0, 0)
-            tr(3, 0)
-            tcp(3, 1, S)
-            t1(0, 1)
+            widen(0, 3, S)
+            trc(2, 1)
             sq(2, 1)
-            t1(1, 2)
-            tcp(3, 0, S)
-            il_cp("x", 0, 0, 0, S)
-            s2(2, 1)
-            il_cp("h", 1, 1, 0, S)
-            t1(1, 1)
-            tr(2, 1)
-            il_cp("h", 1, 1, 1, S)
-            t1(1, 0)
-            pe_da(1, 0, 1)
-            tcp(2, 1, S)
-            pe_da(0, 0, 0)
-            qe(3)
-            il_cp("h", 1, 0, 1, S)
-            pe_da(1, 0, 0)
-            qe(2)
-            pe_da(0, 0, 1)
-            q_w("h", 1, 1)
-            il_cp("h", 0, 0, 1, S)
-            wop(1, 1)
-            il_cp("h", 0, 0, 0, S)
-            wop(0, 1)
-            il_cp("h", 0, 1, 1, S)
-            wop(0, 0)
-            il_cp("h", 1, 0, 0, S)
-            drop(1, 0, 1)
-            drop(0, 0, 0)
-            pe_da(1, 1, 1)
-            widen(1, 0, S)
-            drop(0, 0, 1)
-            pe_da(1, 1, 0)
-            drop(1, 1, 1)
-            widen(1, 2, S)
-            drop(1, 1, 0)
-            drop(1, 0, 0)
+            trc(2, 0)
+            sq(2, 0)
+            trc(3, 1)
+            tra(2, 1, 1)
+            s2(2, 1, 1)
+            tra(2, 1, 0)
+            tra(2, 0, 0)
+            tra(2, 0, 1)
+            trc(3, 0)
+            s2(2, 1, 0)
+            s2(2, 0, 0)
             widen(1, 3, S)
-            wop(1, 0)
+            sq(3, 1)
+            sq(3, 0)
+            widen(1, 0, S)
+            widen(1, 1, S)
+            il_cp("x", 0, 0, S)
+            s2(2, 0, 1)
+            s1(3, 1)
+            s1(3, 0)
+            tra(3, 1, 0)
+            s2(3, 1, 0)
+            tra(3, 0, 0)
+            tra(3, 1, 1)
+            tra(3, 0, 1)
+            widen(1, 2, S)
+            il_cp("x", 1, 1, S)
+            il_cp("h", 0, 0, S)
+            il_cp("h", 0, 3, S)
+            il_cp("x", 1, 0, S)
+            il_cp("x", 0, 1, S)
+            il_cp("h", 1, 0, S)
+            il_cp("h", 1, 1, S)
+            il_cp("h", 0, 1, S)
+            il_cp("h", 1, 2, S)
+            il_cp("h", 0, 2, S)
+            t1(0, 0)
+            s2(3, 0, 0)
+            s2(3, 0, 1)
+            s2(3, 1, 1)
+            pe_da(0, 0, 0)
+            wop(0, 0)
+            qe(2)
+            qe(3)
+            drop(0, 0, 0)
+            pe_da(0, 0, 1)
             pe_da(0, 1, 1)
             pe_da(0, 1, 0)
-            widen(1, 1, S)
-            qdr(1)
-            pe_da(2, 0, 1)
+            drop(0, 0, 1)
+            t1(0, 1)
+            t1(1, 0)
+            t1(1, 1)
+            wop(1, 0)
+            q_w("x", 0)
             drop(0, 1, 0)
-            pe_da(2, 1, 0)
-            il_cp("h", 0, 1, 0, S)
             drop(0, 1, 1)
-            q_w("h", 0, 0)
-            pe_da(2, 1, 1)
-            il_cp("x", 0, 0, 1, S)
+            q_w("x", 1)
             qdr(0)
-            pe_da(3, 1, 0)
-            q_w("h", 0, 1)
-            il_cp("x", 1, 0, 0, S)
-            t1(0, 2)
-            o_mm("h", 1, 2)
-            o_mm("h", 1, 3)
-            o_cp("h", 1, 2, S)
-            q_w("x", 0, 0)
-            o_mm("h", 0, 3)
-            o_cp("h", 1, 3, S)
-            o_mm("h", 0, 2)
-            wop(0, 2)
-            o_cp("h", 0, 3, S)
-            o_st("h", 1, 1)
-            o_cp("h", 0, 2, S)
-            q_w("h", 1, 0)
-            il_cp("x", 1, 1, 0, S)
-            o_st("h", 0, 1)
-            drop(2, 0, 1)
-            o_mm("h", 0, 0)
-            wop(1, 2)
-            o_mm("h", 1, 1)
-            il_cp("x", 1, 0, 1, S)
-            o_mm("h", 0, 1)
-            o_cp("h", 0, 0, V)
-            o_mm("h", 1, 0)
-            drop(2, 1, 0)
-            o_cp("h", 0, 1, S)
-            pe_da(3, 1, 1)
-            q_w("x", 1, 0)
-            o_cp("h", 1, 1, S)
-            o_st("h", 0, 0)
+            wop(1, 1)
+            pe_da(1, 1, 1)
+            pe_da(1, 1, 0)
+            pe_da(1, 0, 0)
+            o_mm("x", (0, 1), (0,))
+            o_mm("x", (2, 3), (0,))
+            wop(0, 1)
+            q_w("h", 0)
+            o_mm("h", (0, 1), (0,))
+            drop(1, 1, 1)
+            pe_da(1, 0, 1)
+            drop(1, 1, 0)
+            drop(1, 0, 0)
+            drop(1, 0, 1)
+            pe_da(2, 0, 1)
+            o_cp("x", (0, 1), (0,), (0, 1, 2, 3), (0,), S)
+            o_cp("x", (2, 3), (0,), (0, 1, 2, 3), (0,), S)
+            il_cp("h", 1, 3, S)
+            il_cp("x", 1, 2, S)
+            il_cp("x", 0, 2, S)
             pe_da(2, 0, 0)
-            il_cp("x", 1, 1, 1, S)
-            o_cp("h", 1, 0, V)
-            o_mm("x", 0, 1)
+            q_w("h", 1)
+            qdr(1)
+            q_w("h", 2)
+            t1(0, 2)
+            q_w("h", 3)
+            wop(0, 2)
+            q_w("x", 2)
+            pe_da(2, 1, 0)
+            o_mm("h", (2, 3), (0,))
+            o_cp("h", (0, 1), (0,), (0, 1, 2, 3), (0,), S)
+            o_mm("h", (2, 3), (1,))
+            o_cp("h", (2, 3), (0,), (0, 1, 2, 3), (0,), S)
+            o_mm("x", (2, 3), (1,))
+            o_mm("h", (0, 1), (1,))
+            o_cp("h", (2, 3), (1,), (0, 1, 2, 3), (1,), S)
+            o_cp("x", (2, 3), (1,), (0, 1, 2, 3), (1,), S)
+            o_cp("h", (0, 1), (1,), (0, 1, 2, 3), (1,), S)
+            o_mm("x", (0, 1), (1,))
+            o_mm("h", (4, 5), (1,))
+            o_mm("h", (6, 7), (1,))
+            t1(1, 2)
+            drop(2, 0, 1)
+            wop(1, 2)
+            il_cp("x", 0, 3, S)
+            o_cp("h", (4, 5), (1,), (4, 5, 6, 7), (1,), S)
+            o_cp("x", (0, 1), (1,), (0, 1, 2, 3), (1,), S)
+            o_mm("h", (4, 5), (0,))
+            o_mm("h", (6, 7), (0,))
+            o_mm("x", (4,), (0, 1))
+            il_cp("x", 1, 3, S)
+            o_cp("h", (6, 7), (1,), (4, 5, 6, 7), (1,), S)
+            o_cp("x", (4,), (0, 1), (4, 5), (0, 1), S)
+            o_cp("h", (6, 7), (0,), (4, 5, 6, 7), (0,), S)
+            o_mm("x", (5,), (0, 1))
+            pe_da(2, 1, 1)
+            o_cp("x", (5,), (0, 1), (4, 5), (0, 1), S)
+            il_cp("x", 0, 4, S)
+            o_cp("h", (4, 5), (0,), (4, 5, 6, 7), (0,), S)
             drop(2, 0, 0)
-            o_st("h", 1, 0)
-            o_mm("x", 0, 0)
+            drop(2, 1, 0)
             drop(2, 1, 1)
-            o_cp("x", 0, 1, S)
-            o_mm("x", 1, 0)
-            q_w("x", 1, 1)
-            o_cp("x", 0, 0, S)
-            o_mm("x", 1, 1)
+            q_w("x", 3)
             qdr(2)
-            o_cp("x", 1, 0, S)
+            pe_da(3, 1, 0)
             pe_da(3, 0, 0)
-            o_st("x", 0, 0)
-            o_cp("x", 1, 1, S)
-            il_cp("x", 0, 1, 0, V)
-            o_mm("h", 2, 1)
-            il_cp("x", 0, 1, 1, V)
-            o_st("x", 1, 0)
-            o_mm("h", 2, 0)
-            o_cp("h", 2, 1, S)
-            o_mm("h", 2, 3)
-            t1(1, 3)
-            o_cp("h", 2, 0, S)
-            o_mm("x", 2, 1)
-            o_cp("h", 2, 3, S)
-            o_st("h", 2, 0)
-            o_mm("h", 2, 2)
-            q_w("x", 0, 1)
-            o_cp("x", 2, 1, S)
-            o_mm("x", 2, 0)
-            wop(1, 3)
-            o_cp("h", 2, 2, S)
-            o_mm("x", 1, 3)
-            o_cp("x", 2, 0, S)
-            o_st("h", 2, 1)
-            o_mm("x", 1, 2)
+            o_mm("x", (6,), (0, 1))
             t1(0, 3)
-            o_cp("x", 1, 3, S)
-            o_st("x", 2, 0)
-            o_mm("x", 0, 2)
-            o_cp("x", 1, 2, S)
-            o_mm("x", 2, 3)
-            o_cp("x", 0, 2, S)
-            drop(3, 1, 0)
-            o_mm("x", 0, 3)
-            o_st("x", 1, 1)
-            o_cp("x", 2, 3, S)
+            t1(1, 3)
             wop(0, 3)
-            o_mm("x", 2, 2)
-            o_cp("x", 0, 3, S)
-            pe_da(3, 0, 1)
-            o_cp("x", 2, 2, S)
-            drop(3, 1, 1)
-            o_st("x", 0, 1)
+            wop(1, 3)
             drop(3, 0, 0)
-            o_st("x", 2, 1)
-            drop(3, 0, 1)
+            drop(3, 1, 0)
+            t1(1, 4)
+            o_cp("x", (6,), (0, 1), (6,), (0, 1), S)
+            o_mm("h", (0, 1), (2,))
+            o_mm("h", (2, 3), (2,))
+            o_st("x", (0, 1, 2, 3), (0,))
+            o_st("h", (0, 1, 2, 3), (0,))
+            o_st("h", (0, 1, 2, 3), (1,))
+            o_st("x", (0, 1, 2, 3), (1,))
+            o_st("h", (4, 5, 6, 7), (1,))
+            o_st("x", (4, 5), (0, 1))
+            o_st("h", (4, 5, 6, 7), (0,))
+            o_st("x", (6,), (0, 1))
+            o_cp("h", (0, 1), (2,), (0, 1, 2, 3), (2,), S)
+            o_cp("h", (2, 3), (2,), (0, 1, 2, 3), (2,), S)
+            o_mm("h", (4, 5), (2,))
+            o_mm("h", (6, 7), (2,))
+            o_mm("x", (2, 3), (2,))
+            pe_da(4, 1, 0)
+            o_mm("x", (0, 1), (2,))
+            o_cp("h", (4, 5), (2,), (4, 5, 6, 7), (2,), S)
+            o_cp("h", (6, 7), (2,), (4, 5, 6, 7), (2,), S)
+            o_cp("x", (2, 3), (2,), (0, 1, 2, 3), (2,), S)
+            il_cp("x", 1, 4, S)
+            o_st("h", (0, 1, 2, 3), (2,))
             qdr(3)
-            o_mm("h", 3, 2)
-            o_mm("x", 3, 2)
-            o_cp("h", 3, 2, S)
-            o_mm("h", 3, 3)
-            o_cp("x", 3, 2, V)
-            o_st("h", 3, 2)
-            o_mm("h", 3, 0)
-            o_cp("h", 3, 3, V)
-            o_st("h", 3, 3)
-            o_mm("h", 3, 1)
-            o_cp("h", 3, 0, V)
-            o_mm("x", 3, 1)
-            o_st("h", 3, 0)
-            o_cp("h", 3, 1, S)
-            o_mm("x", 3, 0)
-            o_st("h", 3, 1)
-            o_cp("x", 3, 1, V)
-            o_st("x", 3, 1)
-            o_mm("x", 3, 3)
-            o_cp("x", 3, 0, V)
-            o_st("x", 3, 0)
-            o_cp("x", 3, 3, S)
-            o_st("x", 3, 3)
-            o_st("x", 3, 2)
+            t1(0, 4)
+            pe_da(4, 0, 0)
+            o_mm("h", (4, 5, 6, 7), (3,))
+            o_cp("x", (0, 1), (2,), (0, 1, 2, 3), (2,), S)
+            wop(1, 4)
+            wop(0, 4)
+            drop(4, 1, 0)
+            o_st("h", (4, 5, 6, 7), (2,))
+            o_cp("h", (4, 5, 6, 7), (3,), (4, 5, 6, 7), (3,), S)
+            o_st("x", (0, 1, 2, 3), (2,))
+            o_st("h", (4, 5, 6, 7), (3,))
+            o_mm("x", (0, 1, 2, 3), (3,))
+            o_mm("h", (0, 1, 2, 3), (3,))
+            o_cp("x", (0, 1, 2, 3), (3,), (0, 1, 2, 3), (3,), S)
+            o_cp("h", (0, 1, 2, 3), (3,), (0, 1, 2, 3), (3,), S)
+            o_st("x", (0, 1, 2, 3), (3,))
+            o_st("h", (0, 1, 2, 3), (3,))
+            drop(4, 0, 0)
+            q_w("x", 4)
+            o_mm("x", (7,), (0, 1))
+            o_cp("x", (7,), (0, 1), (7,), (0, 1), S)
+            o_st("x", (7,), (0, 1))
+            qdr(4)
+            o_mm("x", (0, 1, 2, 3), (4,))
+            o_cp("x", (0, 1, 2, 3), (4,), (0, 1, 2, 3), (4,), V)
+            o_st("x", (0, 1, 2, 3), (4,))
+            o_mm("h", (0, 1, 2, 3), (4,))
+            o_cp("h", (0, 1, 2, 3), (4,), (0, 1, 2, 3), (4,), S)
+            o_st("h", (0, 1, 2, 3), (4,))
+            o_mm("h", (4, 5, 6, 7), (4,))
+            o_cp("h", (4, 5, 6, 7), (4,), (4, 5, 6, 7), (4,), S)
+            o_st("h", (4, 5, 6, 7), (4,))
+            o_mm("x", (6,), (2, 3, 4))
+            o_cp("x", (6,), (2, 3, 4), (6,), (2, 3, 4), S)
+            o_st("x", (6,), (2, 3, 4))
+            o_mm("x", (5,), (2, 3, 4))
+            o_cp("x", (5,), (2, 3, 4), (4, 5), (2, 3, 4), V)
+            o_mm("x", (7,), (2, 3, 4))
+            o_cp("x", (7,), (2, 3, 4), (7,), (2, 3, 4), V)
+            o_st("x", (7,), (2, 3, 4))
+            o_mm("x", (4,), (2, 3, 4))
+            o_cp("x", (4,), (2, 3, 4), (4, 5), (2, 3, 4), V)
+            o_st("x", (4, 5), (2, 3, 4))

@@ -19,7 +19,7 @@ N = 1024
 FLOPS = 3 * 2 * N * N * N
 CW = [256, 256, 256, 128, 128]
 HW = [256, 256, 256, 256]
-XW = [256, 256, 256, 128, 128]
+XW = [256, 256, 256, 256]
 V, S = "v", "s"
 
 
@@ -49,7 +49,7 @@ def tile_gruresetgateweightgradient_w4_kernel(tc, g, z, c, r, h, x_bytes, x_scal
             d, src = {"z": (zt, gz), "g": (gt, gg), "c": (ct, gc)}[nm]
             gi, tp = divmod(pi, 2)
             if pi not in d:
-                d[pi] = pool.tile([P, 2, N], BF16, tag="ld", bufs=13, name=nm + str(pi))
+                d[pi] = pool.tile([P, 2, N], BF16, tag="ld", bufs=12, name=nm + str(pi))
             lo, hi = (0, 2) if t is None else (t, t + 1)
             cols = slice(0, N) if half is None else slice(512 * half, 512 * (half + 1))
             nc.sync.dma_start(out=d[pi][:, lo:hi, cols], in_=src[gi][:, 2 * tp + lo : 2 * tp + hi, cols])
@@ -76,47 +76,39 @@ def tile_gruresetgateweightgradient_w4_kernel(tc, g, z, c, r, h, x_bytes, x_scal
             else:
                 nc.scalar.copy(out=out, in_=in_)
 
-        cb, c2, av, ab, eg, ec, es = {}, {}, {}, {}, {}, {}, {}
-
-        def trc(pi, t):
-            cb[pi, t] = psum.tile([P, 2, 2, P], F32, tag="mm", bufs=5, name="cb_%d%d" % (pi, t))
-            words = ct[pi][:, t, :].bitcast(F32)
-            for k in range(2):
-                for u in range(2):
-                    nc.tensor.transpose(cb[pi, t][:, u, k, :], words[:, 256 * k + u : 256 * (k + 1) : 2], id_f[:])
+        c2, av, eb, xt, eg, ec, es = {}, {}, {}, {}, {}, {}, {}
 
         def sq(pi, t):
-            c2[pi, t] = pool.tile([P, 2, P, 4], F32, tag="c2", bufs=3, name="c2_%d%d" % (pi, t))
-            src = cb[pi, t][:].rearrange("p u k n -> p (u k n)").bitcast(BF16).rearrange("p (u m e) -> p m u e", u=2, e=2)
-            dst = c2[pi, t][:].rearrange("p k n (u e) -> p (k n) u e", e=2)
-            nc.scalar.activation(out=dst, in_=src, func=ACT.Square)
+            c2[pi, t] = pool.tile([P, N], F32, tag="c2", bufs=3, name="c2_%d%d" % (pi, t))
+            nc.scalar.activation(out=c2[pi, t][:], in_=ct[pi][:, t, :], func=ACT.Square)
 
-        def s1(pi, t, k=None):
+        def s1(pi, t, half=None):
             if (pi, t) not in av:
-                av[pi, t] = pool.tile([P, 4, 2 * P], F32, tag="av", bufs=6, name="a_%d%d" % (pi, t))
-            js = slice(0, 2 * P) if k is None else slice(P * k, P * (k + 1))
+                av[pi, t] = pool.tile([P, N], F32, tag="av", bufs=6, name="a_%d%d" % (pi, t))
+            cols = slice(0, N) if half is None else slice(512 * half, 512 * (half + 1))
+            nc.vector.scalar_tensor_tensor(out=av[pi, t][:, cols], in0=zt[pi][:, t, cols], scalar=1.0, in1=gt[pi][:, t, cols], op0=ALU.subtract, op1=ALU.mult)
 
-            def by_u(tile):
-                return tile[:, t, :].rearrange("p (j u) -> p u j", u=4)[:, :, js]
+        def s2(pi, t):
+            eb[pi, t] = pool.tile([P, N], BF16, tag="eb", bufs=3, align_bytes=64, name="e_%d%d" % (pi, t))
+            nc.vector.scalar_tensor_tensor(out=eb[pi, t][:], in0=c2[pi, t][:], scalar=1.0, in1=av[pi, t][:], op0=ALU.subtract, op1=ALU.mult)
 
-            nc.vector.scalar_tensor_tensor(out=av[pi, t][:, :, js], in0=by_u(zt[pi]), scalar=1.0, in1=by_u(gt[pi]), op0=ALU.subtract, op1=ALU.mult)
+        def tr(pi, t):
+            xt[pi, t] = psum.tile([P, 2, 2, P], F32, tag="mm", bufs=4, name="xt_%d%d" % (pi, t))
+            words = eb[pi, t][:].bitcast(F32)
+            for k in range(2):
+                for u in range(2):
+                    nc.tensor.transpose(xt[pi, t][:, k, u, :], words[:, 256 * k + u : 256 * (k + 1) : 2], id_f[:])
 
-        def tra(pi, t, k):
-            ab[pi, t, k] = psum.tile([P, 4, P], F32, tag="da", bufs=3, name="ab_%d%d%d" % (pi, t, k))
-            for u in range(4):
-                nc.tensor.transpose(ab[pi, t, k][:, u, :], av[pi, t][:, u, P * k : P * (k + 1)], id_f[:])
-
-        def s2(pi, t, k):
+        def tcp(pi, t, eng):
             if pi not in eg:
-                eg[pi] = pool.tile([P, 2, 2, P, 4], BF16, tag="eg", bufs=2, align_bytes=64, name="eg_%d" % pi)
-            nc.vector.scalar_tensor_tensor(
-                out=eg[pi][:, t, k], in0=c2[pi, t][:, k], scalar=1.0, in1=ab[pi, t, k][:].rearrange("p u n -> p n u"),
-                op0=ALU.subtract, op1=ALU.mult)
+                eg[pi] = pool.tile([P, 2 * 2 * P * 4], BF16, tag="eg", bufs=2, align_bytes=64, name="eg_%d" % pi)
+            dst = eg[pi][:].bitcast(F32)[:, 512 * t : 512 * (t + 1)].rearrange("p (k m u) -> p k m u", k=2, u=2)
+            copy(eng, dst, xt[pi, t][:].rearrange("p k u m -> p k m u"))
 
         def qe(pi):
             ec[pi] = keep.tile([P, 512], U32, align_bytes=64, name="ec_%d" % pi)
             es[pi] = keep.tile([P, 512], U8, align_bytes=64, name="es_%d" % pi)
-            nc.vector.quantize_mx(out=ec[pi][:].bitcast(FP8X4), scales=es[pi][:], in_=eg[pi][:].rearrange("p t k n u -> p (t k n u)"))
+            nc.vector.quantize_mx(out=ec[pi][:].bitcast(FP8X4), scales=es[pi][:], in_=eg[pi][:])
 
         xb = {}
 
@@ -163,17 +155,19 @@ def tile_gruresetgateweightgradient_w4_kernel(tc, g, z, c, r, h, x_bytes, x_scal
         w = {}
 
         def t1(gi, b):
-            w[gi, b] = pool.tile([P, 4, CW[b]], F32, tag="av", bufs=6, name="w_%d%d" % (gi, b))
-            rr = quad["r", gi][:, :, start("d", b) : start("d", b + 1)]
+            w[gi, b] = pool.tile([P, CW[b], 4], F32, tag="av", bufs=6, name="w_%d%d" % (gi, b))
+            rr = quad["r", gi][:, :, start("d", b) : start("d", b + 1)].rearrange("p t n -> p n t")
             nc.vector.scalar_tensor_tensor(out=w[gi, b][:], in0=rr, scalar=1.0, in1=rr, op0=ALU.subtract, op1=ALU.mult)
 
         def wop(gi, b):
-            nc.vector.tensor_tensor(out=w[gi, b][:], in0=w[gi, b][:], in1=quad["h", gi][:, :, start("d", b) : start("d", b + 1)], op=ALU.mult)
+            a = start("d", b) // HW[0]
+            c0 = start("d", b) - start("h", a)
+            nc.vector.tensor_tensor(out=w[gi, b][:], in0=w[gi, b][:], in1=il["h", a][:, gi, c0 : c0 + CW[b], :], op=ALU.mult)
 
         da = {}
 
         def pe_da(b, gi, j):
-            bank = psum.tile([P, 4, P], F32, tag="da", bufs=3, name="da_%d%d%d" % (b, gi, j))
+            bank = psum.tile([P, 4, P], F32, tag="da", bufs=4, name="da_%d%d%d" % (b, gi, j))
             da[b, gi, j] = bank
             i0 = start("d", b) + P * j
             for t in range(4):
@@ -193,7 +187,7 @@ def tile_gruresetgateweightgradient_w4_kernel(tc, g, z, c, r, h, x_bytes, x_scal
                 dr[b] = pool.tile([P, 2, CW[b], 4], BF16, tag="dr", bufs=2, align_bytes=64, name="dr_%d" % b)
             nc.vector.scalar_tensor_tensor(
                 out=dr[b][:, gi, P * j : P * (j + 1), :], in0=da[b, gi, j][:].rearrange("p t n -> p n t"), scalar=-1.0,
-                in1=w[gi, b][:, :, P * j : P * (j + 1)].rearrange("p t n -> p n t"), op0=ALU.mult, op1=ALU.mult)
+                in1=w[gi, b][:, P * j : P * (j + 1), :], op0=ALU.mult, op1=ALU.mult)
 
         def qdr(b):
             quantize("d", b, dr[b])
@@ -201,7 +195,7 @@ def tile_gruresetgateweightgradient_w4_kernel(tc, g, z, c, r, h, x_bytes, x_scal
         obank, res = {}, {}
 
         def o_mm(nm, ms, bs):
-            bank = psum.tile([P, len(ms), sum(CW[b] for b in bs)], F32, tag="mm", bufs=5, name="o_%s%d_%d" % (nm, ms[0], bs[0]))
+            bank = psum.tile([P, len(ms), sum(CW[b] for b in bs)], F32, tag="mm", bufs=4, name="o_%s%d_%d" % (nm, ms[0], bs[0]))
             obank[nm, ms[0], bs[0]] = bank
             for i, m in enumerate(ms):
                 a = max(k for k in range(len(width[nm])) if start(nm, k) <= P * m)
@@ -219,7 +213,7 @@ def tile_gruresetgateweightgradient_w4_kernel(tc, g, z, c, r, h, x_bytes, x_scal
         def o_cp(nm, ms, bs, st_ms, st_bs, eng):
             key = (nm, st_ms[0], st_bs[0])
             if key not in res:
-                res[key] = pool.tile([P, len(st_ms), sum(CW[b] for b in st_bs)], F32, tag="ld", bufs=13, name="r_%s%d_%d" % key)
+                res[key] = pool.tile([P, len(st_ms), sum(CW[b] for b in st_bs)], F32, tag="ld", bufs=12, name="r_%s%d_%d" % key)
             i0, c0 = st_ms.index(ms[0]), start("d", bs[0]) - start("d", st_bs[0])
             copy(eng, res[key][:, i0 : i0 + len(ms), c0 : c0 + sum(CW[b] for b in bs)], obank[nm, ms[0], bs[0]][:])
 
@@ -233,265 +227,244 @@ def tile_gruresetgateweightgradient_w4_kernel(tc, g, z, c, r, h, x_bytes, x_scal
         with tc.manual_schedule():
             nc.scalar.activation(out=zero[:], in_=zero[:], func=ACT.Square)
             load_zgc("c", 0, 0)
-            trc(0, 0)
             sq(0, 0)
+            load_zgc("g", 0, 0, 0)
+            load_zgc("z", 0, 0, 0)
+            s1(0, 0, 0)
             load_zgc("z", 0, 0, 1)
             load_zgc("g", 0, 0, 1)
             s1(0, 0, 1)
-            tra(0, 0, 1)
-            s2(0, 0, 1)
-            load_zgc("z", 0, 1)
-            load_zgc("c", 0, 1)
+            s2(0, 0)
+            tr(0, 0)
             load_zgc("g", 0, 1)
-            trc(0, 1)
-            sq(0, 1)
+            load_zgc("c", 0, 1)
+            load_zgc("z", 0, 1)
             s1(0, 1)
-            load_zgc("z", 0, 0, 0)
-            load_zgc("g", 0, 0, 0)
-            s1(0, 0, 0)
-            tra(0, 1, 0)
-            s2(0, 1, 0)
-            tra(0, 1, 1)
-            s2(0, 1, 1)
-            tra(0, 0, 0)
-            s2(0, 0, 0)
-            qe(0)
-            load_zgc("c", 1, None)
+            sq(0, 1)
+            s2(0, 1)
+            tr(0, 1)
             load_zgc("z", 1, None)
             load_zgc("g", 1, None)
-            trc(1, 1)
-            trc(1, 0)
-            s1(1, 0)
+            load_zgc("c", 1, None)
+            load_zgc("g", 2, None)
             load_xs()
             load_x(0)
-            load_zgc("g", 2, None)
             load_zgc("z", 2, None)
             load_zgc("c", 2, None)
-            load_zgc("c", 3, None)
-            load_x(1)
-            load_zgc("g", 3, None)
             load_zgc("z", 3, None)
             load_quad("r", 0)
+            load_zgc("g", 3, None)
+            load_zgc("c", 3, None)
             load_quad("h", 0)
             load_us(0), load_us(1), load_us(2), load_us(3), load_uw()
-            load_quad("r", 1)
             load_quad("h", 1)
-            s1(1, 1)
+            load_quad("r", 1)
+            load_x(1)
+            tcp(0, 0, S)
             sq(1, 1)
             sq(1, 0)
-            tra(1, 0, 0)
-            tra(1, 0, 1)
-            s2(1, 0, 0)
-            s2(1, 0, 1)
-            tra(1, 1, 0)
-            s2(1, 1, 0)
-            tra(1, 1, 1)
-            s1(2, 1)
-            s2(1, 1, 1)
-            s1(2, 0)
-            qe(1)
-            widen(0, 2, S)
+            tcp(0, 1, S)
             widen(0, 1, S)
+            widen(0, 2, S)
+            s1(1, 1)
+            s1(1, 0)
+            s2(1, 1)
+            s2(1, 0)
+            qe(0)
+            s1(2, 0)
+            s1(2, 1)
+            sq(2, 0)
+            s2(2, 0)
+            tr(1, 0)
+            tr(1, 1)
+            tr(2, 0)
+            sq(2, 1)
             widen(0, 0, S)
             widen(0, 3, S)
-            trc(2, 1)
-            sq(2, 1)
-            trc(2, 0)
-            sq(2, 0)
-            trc(3, 1)
-            tra(2, 1, 1)
-            s2(2, 1, 1)
-            tra(2, 1, 0)
-            tra(2, 0, 0)
-            tra(2, 0, 1)
-            trc(3, 0)
-            s2(2, 1, 0)
-            s2(2, 0, 0)
-            widen(1, 3, S)
-            sq(3, 1)
-            sq(3, 0)
-            widen(1, 0, S)
-            widen(1, 1, S)
-            il_cp("x", 0, 0, S)
-            s2(2, 0, 1)
+            tcp(1, 0, S)
+            tcp(1, 1, S)
+            tcp(2, 0, S)
+            s2(2, 1)
+            t1(0, 0)
             s1(3, 1)
             s1(3, 0)
-            tra(3, 1, 0)
-            s2(3, 1, 0)
-            tra(3, 0, 0)
-            tra(3, 1, 1)
-            tra(3, 0, 1)
-            widen(1, 2, S)
-            il_cp("x", 1, 1, S)
+            qe(1)
+            sq(3, 0)
+            sq(3, 1)
+            tr(2, 1)
+            s2(3, 0)
+            s2(3, 1)
+            tr(3, 0)
+            tr(3, 1)
+            pe_da(1, 0, 0)
+            pe_da(1, 0, 1)
+            pe_da(0, 0, 1)
+            pe_da(0, 0, 0)
             il_cp("h", 0, 0, S)
-            il_cp("h", 0, 3, S)
-            il_cp("x", 1, 0, S)
+            tcp(2, 1, S)
+            il_cp("h", 0, 1, S)
+            tcp(3, 1, S)
+            tcp(3, 0, S)
+            t1(0, 1)
+            wop(0, 0)
+            wop(0, 1)
+            qe(3)
+            drop(1, 0, 1)
+            qe(2)
+            drop(1, 0, 0)
+            t1(1, 1)
             il_cp("x", 0, 1, S)
             il_cp("h", 1, 0, S)
             il_cp("h", 1, 1, S)
-            il_cp("h", 0, 1, S)
-            il_cp("h", 1, 2, S)
-            il_cp("h", 0, 2, S)
-            t1(0, 0)
-            s2(3, 0, 0)
-            s2(3, 0, 1)
-            s2(3, 1, 1)
-            pe_da(0, 0, 0)
-            wop(0, 0)
-            qe(2)
-            qe(3)
-            drop(0, 0, 0)
-            pe_da(0, 0, 1)
-            pe_da(0, 1, 1)
-            pe_da(0, 1, 0)
             drop(0, 0, 1)
-            t1(0, 1)
+            pe_da(1, 1, 0)
+            pe_da(1, 1, 1)
+            wop(1, 1)
+            drop(0, 0, 0)
+            drop(1, 1, 0)
+            drop(1, 1, 1)
+            q_w("h", 0)
+            qdr(1)
+            pe_da(0, 1, 0)
+            widen(1, 0, S)
+            widen(1, 2, S)
+            widen(1, 1, S)
+            widen(1, 3, S)
+            il_cp("x", 1, 0, S)
+            pe_da(0, 1, 1)
+            pe_da(2, 0, 0)
+            pe_da(2, 1, 1)
+            o_mm("h", (0, 1), (1,))
+            il_cp("x", 1, 1, S)
+            o_cp("h", (0, 1), (1,), (0, 1, 2, 3), (1,), S)
+            il_cp("x", 0, 0, S)
             t1(1, 0)
-            t1(1, 1)
+            q_w("h", 1)
             wop(1, 0)
-            q_w("x", 0)
+            q_w("x", 1)
             drop(0, 1, 0)
             drop(0, 1, 1)
-            q_w("x", 1)
+            q_w("x", 0)
             qdr(0)
-            wop(1, 1)
-            pe_da(1, 1, 1)
-            pe_da(1, 1, 0)
-            pe_da(1, 0, 0)
-            o_mm("x", (0, 1), (0,))
-            o_mm("x", (2, 3), (0,))
-            wop(0, 1)
-            q_w("h", 0)
-            o_mm("h", (0, 1), (0,))
-            drop(1, 1, 1)
-            pe_da(1, 0, 1)
-            drop(1, 1, 0)
-            drop(1, 0, 0)
-            drop(1, 0, 1)
-            pe_da(2, 0, 1)
-            o_cp("x", (0, 1), (0,), (0, 1, 2, 3), (0,), S)
-            o_cp("x", (2, 3), (0,), (0, 1, 2, 3), (0,), S)
-            il_cp("h", 1, 3, S)
-            il_cp("x", 1, 2, S)
-            il_cp("x", 0, 2, S)
-            pe_da(2, 0, 0)
-            q_w("h", 1)
-            qdr(1)
-            q_w("h", 2)
             t1(0, 2)
-            q_w("h", 3)
-            wop(0, 2)
-            q_w("x", 2)
-            pe_da(2, 1, 0)
-            o_mm("h", (2, 3), (0,))
-            o_cp("h", (0, 1), (0,), (0, 1, 2, 3), (0,), S)
-            o_mm("h", (2, 3), (1,))
-            o_cp("h", (2, 3), (0,), (0, 1, 2, 3), (0,), S)
-            o_mm("x", (2, 3), (1,))
-            o_mm("h", (0, 1), (1,))
-            o_cp("h", (2, 3), (1,), (0, 1, 2, 3), (1,), S)
-            o_cp("x", (2, 3), (1,), (0, 1, 2, 3), (1,), S)
-            o_cp("h", (0, 1), (1,), (0, 1, 2, 3), (1,), S)
-            o_mm("x", (0, 1), (1,))
-            o_mm("h", (4, 5), (1,))
-            o_mm("h", (6, 7), (1,))
             t1(1, 2)
-            drop(2, 0, 1)
-            wop(1, 2)
-            il_cp("x", 0, 3, S)
-            o_cp("h", (4, 5), (1,), (4, 5, 6, 7), (1,), S)
+            o_mm("h", (2, 3), (1,))
+            o_mm("x", (2, 3), (1,))
+            o_cp("h", (2, 3), (1,), (0, 1, 2, 3), (1,), S)
+            pe_da(2, 1, 0)
+            o_mm("x", (0, 1), (1,))
+            o_mm("h", (0, 1), (0,))
+            o_mm("h", (2, 3), (0,))
+            il_cp("h", 0, 2, S)
+            o_cp("x", (2, 3), (1,), (0, 1, 2, 3), (1,), S)
+            il_cp("h", 1, 2, S)
+            wop(0, 2)
             o_cp("x", (0, 1), (1,), (0, 1, 2, 3), (1,), S)
-            o_mm("h", (4, 5), (0,))
-            o_mm("h", (6, 7), (0,))
-            o_mm("x", (4,), (0, 1))
-            il_cp("x", 1, 3, S)
-            o_cp("h", (6, 7), (1,), (4, 5, 6, 7), (1,), S)
-            o_cp("x", (4,), (0, 1), (4, 5), (0, 1), S)
-            o_cp("h", (6, 7), (0,), (4, 5, 6, 7), (0,), S)
-            o_mm("x", (5,), (0, 1))
-            pe_da(2, 1, 1)
-            o_cp("x", (5,), (0, 1), (4, 5), (0, 1), S)
-            il_cp("x", 0, 4, S)
-            o_cp("h", (4, 5), (0,), (4, 5, 6, 7), (0,), S)
+            o_cp("h", (0, 1), (0,), (0, 1, 2, 3), (0,), S)
+            il_cp("h", 1, 3, S)
+            o_cp("h", (2, 3), (0,), (0, 1, 2, 3), (0,), S)
+            il_cp("h", 0, 3, S)
+            q_w("h", 2)
             drop(2, 0, 0)
-            drop(2, 1, 0)
-            drop(2, 1, 1)
-            q_w("x", 3)
-            qdr(2)
+            wop(1, 2)
+            q_w("h", 3)
+            o_mm("x", (2, 3), (0,))
+            pe_da(2, 0, 1)
+            o_mm("x", (0, 1), (0,))
+            o_mm("h", (4, 5), (1,))
             pe_da(3, 1, 0)
-            pe_da(3, 0, 0)
-            o_mm("x", (6,), (0, 1))
+            o_mm("h", (4, 5), (0,))
+            o_cp("x", (2, 3), (0,), (0, 1, 2, 3), (0,), S)
+            o_cp("x", (0, 1), (0,), (0, 1, 2, 3), (0,), S)
+            o_cp("h", (4, 5), (1,), (4, 5, 6, 7), (1,), S)
+            o_cp("h", (4, 5), (0,), (4, 5, 6, 7), (0,), S)
+            drop(2, 0, 1)
+            drop(2, 1, 1)
+            drop(2, 1, 0)
+            qdr(2)
             t1(0, 3)
             t1(1, 3)
             wop(0, 3)
             wop(1, 3)
-            drop(3, 0, 0)
-            drop(3, 1, 0)
-            t1(1, 4)
-            o_cp("x", (6,), (0, 1), (6,), (0, 1), S)
-            o_mm("h", (0, 1), (2,))
-            o_mm("h", (2, 3), (2,))
-            o_st("x", (0, 1, 2, 3), (0,))
-            o_st("h", (0, 1, 2, 3), (0,))
             o_st("h", (0, 1, 2, 3), (1,))
             o_st("x", (0, 1, 2, 3), (1,))
-            o_st("h", (4, 5, 6, 7), (1,))
-            o_st("x", (4, 5), (0, 1))
+            o_st("h", (0, 1, 2, 3), (0,))
+            o_st("x", (0, 1, 2, 3), (0,))
+            o_mm("h", (6, 7), (0,))
+            o_mm("h", (6, 7), (1,))
+            pe_da(3, 0, 0)
+            pe_da(4, 0, 0)
+            o_cp("h", (6, 7), (0,), (4, 5, 6, 7), (0,), S)
             o_st("h", (4, 5, 6, 7), (0,))
-            o_st("x", (6,), (0, 1))
+            o_cp("h", (6, 7), (1,), (4, 5, 6, 7), (1,), S)
+            il_cp("x", 0, 2, S)
+            o_st("h", (4, 5, 6, 7), (1,))
+            o_mm("h", (0, 1), (2,))
             o_cp("h", (0, 1), (2,), (0, 1, 2, 3), (2,), S)
+            o_mm("h", (2, 3), (2,))
             o_cp("h", (2, 3), (2,), (0, 1, 2, 3), (2,), S)
+            o_st("h", (0, 1, 2, 3), (2,))
             o_mm("h", (4, 5), (2,))
             o_mm("h", (6, 7), (2,))
+            o_mm("x", (0, 1), (2,))
             o_mm("x", (2, 3), (2,))
             pe_da(4, 1, 0)
-            o_mm("x", (0, 1), (2,))
             o_cp("h", (4, 5), (2,), (4, 5, 6, 7), (2,), S)
             o_cp("h", (6, 7), (2,), (4, 5, 6, 7), (2,), S)
-            o_cp("x", (2, 3), (2,), (0, 1, 2, 3), (2,), S)
-            il_cp("x", 1, 4, S)
-            o_st("h", (0, 1, 2, 3), (2,))
-            qdr(3)
-            t1(0, 4)
-            pe_da(4, 0, 0)
-            o_mm("h", (4, 5, 6, 7), (3,))
             o_cp("x", (0, 1), (2,), (0, 1, 2, 3), (2,), S)
-            wop(1, 4)
-            wop(0, 4)
-            drop(4, 1, 0)
+            o_cp("x", (2, 3), (2,), (0, 1, 2, 3), (2,), S)
             o_st("h", (4, 5, 6, 7), (2,))
-            o_cp("h", (4, 5, 6, 7), (3,), (4, 5, 6, 7), (3,), S)
-            o_st("x", (0, 1, 2, 3), (2,))
-            o_st("h", (4, 5, 6, 7), (3,))
-            o_mm("x", (0, 1, 2, 3), (3,))
-            o_mm("h", (0, 1, 2, 3), (3,))
-            o_cp("x", (0, 1, 2, 3), (3,), (0, 1, 2, 3), (3,), S)
-            o_cp("h", (0, 1, 2, 3), (3,), (0, 1, 2, 3), (3,), S)
-            o_st("x", (0, 1, 2, 3), (3,))
-            o_st("h", (0, 1, 2, 3), (3,))
+            il_cp("x", 1, 2, S)
+            drop(3, 0, 0)
+            drop(3, 1, 0)
+            t1(0, 4)
+            qdr(3)
+            t1(1, 4)
+            wop(0, 4)
+            wop(1, 4)
+            q_w("x", 2)
+            drop(4, 1, 0)
             drop(4, 0, 0)
-            q_w("x", 4)
-            o_mm("x", (7,), (0, 1))
-            o_cp("x", (7,), (0, 1), (7,), (0, 1), S)
-            o_st("x", (7,), (0, 1))
             qdr(4)
-            o_mm("x", (0, 1, 2, 3), (4,))
-            o_cp("x", (0, 1, 2, 3), (4,), (0, 1, 2, 3), (4,), V)
-            o_st("x", (0, 1, 2, 3), (4,))
-            o_mm("h", (0, 1, 2, 3), (4,))
-            o_cp("h", (0, 1, 2, 3), (4,), (0, 1, 2, 3), (4,), S)
-            o_st("h", (0, 1, 2, 3), (4,))
+            o_mm("x", (0, 1, 2, 3), (3,))
+            o_mm("h", (4, 5, 6, 7), (3,))
+            o_mm("h", (0, 1, 2, 3), (3,))
+            o_st("x", (0, 1, 2, 3), (2,))
+            o_cp("x", (0, 1, 2, 3), (3,), (0, 1, 2, 3), (3,), S)
+            o_cp("h", (4, 5, 6, 7), (3,), (4, 5, 6, 7), (3,), S)
+            o_cp("h", (0, 1, 2, 3), (3,), (0, 1, 2, 3), (3,), S)
+            o_mm("x", (4,), (0, 1))
+            o_mm("x", (5,), (0, 1))
+            o_cp("x", (4,), (0, 1), (4, 5), (0, 1), S)
+            o_cp("x", (5,), (0, 1), (4, 5), (0, 1), S)
+            o_st("x", (0, 1, 2, 3), (3,))
+            o_st("h", (4, 5, 6, 7), (3,))
+            o_st("h", (0, 1, 2, 3), (3,))
+            o_st("x", (4, 5), (0, 1))
             o_mm("h", (4, 5, 6, 7), (4,))
             o_cp("h", (4, 5, 6, 7), (4,), (4, 5, 6, 7), (4,), S)
+            o_mm("h", (0, 1, 2, 3), (4,))
+            o_cp("h", (0, 1, 2, 3), (4,), (0, 1, 2, 3), (4,), S)
             o_st("h", (4, 5, 6, 7), (4,))
-            o_mm("x", (6,), (2, 3, 4))
-            o_cp("x", (6,), (2, 3, 4), (6,), (2, 3, 4), S)
-            o_st("x", (6,), (2, 3, 4))
-            o_mm("x", (5,), (2, 3, 4))
-            o_cp("x", (5,), (2, 3, 4), (4, 5), (2, 3, 4), V)
-            o_mm("x", (7,), (2, 3, 4))
-            o_cp("x", (7,), (2, 3, 4), (7,), (2, 3, 4), V)
-            o_st("x", (7,), (2, 3, 4))
+            o_st("h", (0, 1, 2, 3), (4,))
             o_mm("x", (4,), (2, 3, 4))
-            o_cp("x", (4,), (2, 3, 4), (4, 5), (2, 3, 4), V)
+            o_mm("x", (5,), (2, 3, 4))
+            o_cp("x", (4,), (2, 3, 4), (4, 5), (2, 3, 4), S)
+            o_cp("x", (5,), (2, 3, 4), (4, 5), (2, 3, 4), S)
             o_st("x", (4, 5), (2, 3, 4))
+            o_mm("x", (0, 1, 2, 3), (4,))
+            o_cp("x", (0, 1, 2, 3), (4,), (0, 1, 2, 3), (4,), S)
+            o_st("x", (0, 1, 2, 3), (4,))
+            il_cp("x", 1, 3, V)
+            il_cp("x", 0, 3, V)
+            q_w("x", 3)
+            o_mm("x", (6,), (0, 1))
+            o_mm("x", (7,), (0, 1))
+            o_cp("x", (6,), (0, 1), (6, 7), (0, 1), V)
+            o_cp("x", (7,), (0, 1), (6, 7), (0, 1), V)
+            o_st("x", (6, 7), (0, 1))
+            o_mm("x", (6,), (2, 3, 4))
+            o_cp("x", (6,), (2, 3, 4), (6, 7), (2, 3, 4), V)
+            o_mm("x", (7,), (2, 3, 4))
+            o_cp("x", (7,), (2, 3, 4), (6, 7), (2, 3, 4), S)
+            o_st("x", (6, 7), (2, 3, 4))

from contextlib import ExitStack

import concourse.mybir as mybir
from concourse.masks import make_identity

F32 = mybir.dt.float32
BF16 = mybir.dt.bfloat16
I32 = mybir.dt.int32
U32 = mybir.dt.uint32
U8 = mybir.dt.uint8
FP8 = mybir.dt.float8_e4m3fn
FP8X4 = mybir.dt.float8_e4m3fn_x4
FP4X4 = mybir.dt.float4_e2m1fn_x4
ALU = mybir.AluOpType
ACT = mybir.ActivationFunctionType

P = 128
N = 1024
FLOPS = 3 * 2 * N * N * N
CW = [256, 256, 256, 128, 128]
HW = [256, 256, 256, 256]
XW = [256, 256, 256, 256]
V, S = "v", "s"


def tile_gruresetgateweightgradient_w4_kernel(tc, g, z, c, r, h, x_bytes, x_scale, uc_words, uc_scales, out_0, out_1):
    nc = tc.nc
    with ExitStack() as ctx:
        keep = ctx.enter_context(tc.tile_pool(name="keep", bufs=1))
        pool = ctx.enter_context(tc.tile_pool(name="pool", bufs=2))
        psum = ctx.enter_context(tc.psum_pool(name="psum", bufs=4))

        id_f = keep.tile([P, P], F32, name="id_f")
        ucw = keep.tile([P, 2, 2 * N], U8, align_bytes=64, name="ucw")
        ucs = keep.tile([P, 2, N], U8, align_bytes=64, name="ucs")
        xs = keep.tile([P, 2, 4], F32, name="xs")
        zero = keep.tile([P, 1], F32, name="zero")
        make_identity(nc, id_f[:])

        def rows(ap):
            return ap.rearrange("(g p t) i -> g p t i", g=2, p=P, t=4)

        gz, gg, gc, gr, gh = rows(z), rows(g), rows(c), rows(r), rows(h)
        xv = x_bytes.rearrange("(g p t) i -> g p (t i)", g=2, p=P, t=4)

        zt, gt, ct = {}, {}, {}

        def load_zgc(nm, pi, t, half=None):
            d, src = {"z": (zt, gz), "g": (gt, gg), "c": (ct, gc)}[nm]
            gi, tp = divmod(pi, 2)
            if pi not in d:
                d[pi] = pool.tile([P, 2, N], BF16, tag="ld", bufs=12, name=nm + str(pi))
            lo, hi = (0, 2) if t is None else (t, t + 1)
            cols = slice(0, N) if half is None else slice(512 * half, 512 * (half + 1))
            nc.sync.dma_start(out=d[pi][:, lo:hi, cols], in_=src[gi][:, 2 * tp + lo : 2 * tp + hi, cols])

        def load_uw():
            nc.sync.dma_start(out=ucw[:], in_=uc_words.rearrange("k p n -> p k n"))

        def load_us(q):
            nc.sync.dma_start(out=ucs[32 * q : 32 * q + 4, :, :].bitcast(I32), in_=uc_scales[:, 4 * q : 4 * q + 4, :].rearrange("k q n -> q k n").bitcast(I32))

        def load_xs():
            nc.sync.dma_start(out=xs[:], in_=x_scale.rearrange("(g p t) o -> p g (t o)", g=2, p=P, t=4))

        quad = {}

        def load_quad(nm, gi):
            src = gh if nm == "h" else gr
            quad[nm, gi] = pool.tile([P, 4, N], BF16, tag=nm + "4", bufs=2, name=nm + str(gi))
            nc.sync.dma_start(out=quad[nm, gi][:], in_=src[gi])

        def copy(eng, out, in_):
            if eng == V:
                nc.vector.tensor_copy(out=out, in_=in_)
            else:
                nc.scalar.copy(out=out, in_=in_)

        c2, av, eb, xt, eg, ec, es = {}, {}, {}, {}, {}, {}, {}

        def sq(pi, t):
            c2[pi, t] = pool.tile([P, N], F32, tag="c2", bufs=3, name="c2_%d%d" % (pi, t))
            nc.scalar.activation(out=c2[pi, t][:], in_=ct[pi][:, t, :], func=ACT.Square)

        def s1(pi, t, half=None):
            if (pi, t) not in av:
                av[pi, t] = pool.tile([P, N], F32, tag="av", bufs=6, name="a_%d%d" % (pi, t))
            cols = slice(0, N) if half is None else slice(512 * half, 512 * (half + 1))
            nc.vector.scalar_tensor_tensor(out=av[pi, t][:, cols], in0=zt[pi][:, t, cols], scalar=1.0, in1=gt[pi][:, t, cols], op0=ALU.subtract, op1=ALU.mult)

        def s2(pi, t):
            eb[pi, t] = pool.tile([P, N], BF16, tag="eb", bufs=3, align_bytes=64, name="e_%d%d" % (pi, t))
            nc.vector.scalar_tensor_tensor(out=eb[pi, t][:], in0=c2[pi, t][:], scalar=1.0, in1=av[pi, t][:], op0=ALU.subtract, op1=ALU.mult)

        def tr(pi, t):
            xt[pi, t] = psum.tile([P, 2, 2, P], F32, tag="mm", bufs=4, name="xt_%d%d" % (pi, t))
            words = eb[pi, t][:].bitcast(F32)
            for k in range(2):
                for u in range(2):
                    nc.tensor.transpose(xt[pi, t][:, k, u, :], words[:, 256 * k + u : 256 * (k + 1) : 2], id_f[:])

        def tcp(pi, t, eng):
            if pi not in eg:
                eg[pi] = pool.tile([P, 2 * 2 * P * 4], BF16, tag="eg", bufs=2, align_bytes=64, name="eg_%d" % pi)
            dst = eg[pi][:].bitcast(F32)[:, 512 * t : 512 * (t + 1)].rearrange("p (k m u) -> p k m u", k=2, u=2)
            copy(eng, dst, xt[pi, t][:].rearrange("p k u m -> p k m u"))

        def qe(pi):
            ec[pi] = keep.tile([P, 512], U32, align_bytes=64, name="ec_%d" % pi)
            es[pi] = keep.tile([P, 512], U8, align_bytes=64, name="es_%d" % pi)
            nc.vector.quantize_mx(out=ec[pi][:].bitcast(FP8X4), scales=es[pi][:], in_=eg[pi][:])

        xb = {}

        def load_x(gi):
            xb[gi] = keep.tile([P, 4 * N], U8, align_bytes=64, name="xb_%d" % gi)
            nc.sync.dma_start(out=xb[gi][:], in_=xv[gi])

        def widen(gi, t, eng):
            if ("x", gi) not in quad:
                quad["x", gi] = pool.tile([P, 4, N], BF16, tag="x4", bufs=2, name="x" + str(gi))
            src = xb[gi][:, N * t : N * (t + 1)].bitcast(FP8)
            if eng == V:
                nc.vector.tensor_scalar(out=quad["x", gi][:, t, :], in0=src, scalar1=xs[:, gi, t : t + 1], scalar2=None, op0=ALU.mult)
            else:
                nc.scalar.activation(out=quad["x", gi][:, t, :], in_=src, func=ACT.Copy, scale=xs[:, gi, t : t + 1])

        il = {}
        width = {"h": HW, "x": XW, "d": CW}

        def il_cp(nm, gi, b, eng):
            cw = width[nm][b]
            if (nm, b) not in il:
                il[nm, b] = pool.tile([P, 2, cw, 4], BF16, tag="il" + nm, bufs=2 if nm == "x" else 4, align_bytes=64, name="il_%s%d" % (nm, b))
            c0 = sum(width[nm][:b])
            dst = il[nm, b][:, gi].rearrange("p (c i) t -> p c t i", i=4)
            copy(eng, dst, quad[nm, gi][:, :, c0 : c0 + cw].rearrange("p t (c i) -> p c t i", i=4))

        qc, qs = {}, {}

        def quantize(nm, b, src):
            cw = width[nm][b]
            qc[nm, b] = keep.tile([P, 2, cw], U32, align_bytes=64, name="qc_%s%d" % (nm, b))
            qs[nm, b] = keep.tile([P, 2, cw], U8, align_bytes=64, name="qs_%s%d" % (nm, b))
            nc.vector.quantize_mx(
                out=qc[nm, b][:].rearrange("p g n -> p (g n)").bitcast(FP8X4), scales=qs[nm, b][:].rearrange("p g n -> p (g n)"),
                in_=src[:].rearrange("p g n t -> p (g n t)"))

        def q_w(nm, b):
            quantize(nm, b, il[nm, b])

        def start(nm, b):
            return sum(width[nm][:b])

        w = {}

        def t1(gi, b):
            w[gi, b] = pool.tile([P, CW[b], 4], F32, tag="av", bufs=6, name="w_%d%d" % (gi, b))
            rr = quad["r", gi][:, :, start("d", b) : start("d", b + 1)].rearrange("p t n -> p n t")
            nc.vector.scalar_tensor_tensor(out=w[gi, b][:], in0=rr, scalar=1.0, in1=rr, op0=ALU.subtract, op1=ALU.mult)

        def wop(gi, b):
            a = start("d", b) // HW[0]
            c0 = start("d", b) - start("h", a)
            nc.vector.tensor_tensor(out=w[gi, b][:], in0=w[gi, b][:], in1=il["h", a][:, gi, c0 : c0 + CW[b], :], op=ALU.mult)

        da = {}

        def pe_da(b, gi, j):
            bank = psum.tile([P, 4, P], F32, tag="da", bufs=4, name="da_%d%d%d" % (b, gi, j))
            da[b, gi, j] = bank
            i0 = start("d", b) + P * j
            for t in range(4):
                pi = 2 * gi + t // 2
                for k in range(2):
                    o = P * (2 * (t % 2) + k)
                    nc.tensor.matmul_mx(
                        out=bank[:, t, :],
                        lhsT=ec[pi][:, o : o + P].bitcast(FP8X4), lhsT_scale=es[pi][:, o : o + P],
                        rhs=ucw[:, k, 2 * i0 : 2 * (i0 + P)].bitcast(FP4X4), rhs_scale=ucs[:, k, i0 : i0 + P],
                        start=(k == 0), stop=(k == 1))

        dr = {}

        def drop(b, gi, j):
            if b not in dr:
                dr[b] = pool.tile([P, 2, CW[b], 4], BF16, tag="dr", bufs=2, align_bytes=64, name="dr_%d" % b)
            nc.vector.scalar_tensor_tensor(
                out=dr[b][:, gi, P * j : P * (j + 1), :], in0=da[b, gi, j][:].rearrange("p t n -> p n t"), scalar=-1.0,
                in1=w[gi, b][:, P * j : P * (j + 1), :], op0=ALU.mult, op1=ALU.mult)

        def qdr(b):
            quantize("d", b, dr[b])

        obank, res = {}, {}

        def o_mm(nm, ms, bs):
            bank = psum.tile([P, len(ms), sum(CW[b] for b in bs)], F32, tag="mm", bufs=4, name="o_%s%d_%d" % (nm, ms[0], bs[0]))
            obank[nm, ms[0], bs[0]] = bank
            for i, m in enumerate(ms):
                a = max(k for k in range(len(width[nm])) if start(nm, k) <= P * m)
                rows_m = slice(P * m - start(nm, a), P * (m + 1) - start(nm, a))
                c0 = 0
                for b in bs:
                    for gi in range(2):
                        nc.tensor.matmul_mx(
                            out=bank[:, i, c0 : c0 + CW[b]],
                            lhsT=qc[nm, a][:, gi, rows_m].bitcast(FP8X4), lhsT_scale=qs[nm, a][:, gi, rows_m],
                            rhs=qc["d", b][:, gi, :].bitcast(FP8X4), rhs_scale=qs["d", b][:, gi, :],
                            start=(gi == 0), stop=(gi == 1))
                    c0 += CW[b]

        def o_cp(nm, ms, bs, st_ms, st_bs, eng):
            key = (nm, st_ms[0], st_bs[0])
            if key not in res:
                res[key] = pool.tile([P, len(st_ms), sum(CW[b] for b in st_bs)], F32, tag="ld", bufs=12, name="r_%s%d_%d" % key)
            i0, c0 = st_ms.index(ms[0]), start("d", bs[0]) - start("d", st_bs[0])
            copy(eng, res[key][:, i0 : i0 + len(ms), c0 : c0 + sum(CW[b] for b in bs)], obank[nm, ms[0], bs[0]][:])

        def o_st(nm, ms, bs):
            dst = out_0 if nm == "h" else out_1
            dst = dst[P * ms[0] : P * (ms[-1] + 1), start("d", bs[0]) : start("d", bs[-1] + 1)]
            nc.sync.dma_start(out=dst.rearrange("(m p) i -> p m i", p=P), in_=res[nm, ms[0], bs[0]][:])

        nc.gpsimd.memset(zero[:], 0.0)
        nc.gpsimd.memset(ucs[:].rearrange("p k n -> p (k n)").bitcast(U32), 0)
        with tc.manual_schedule():
            nc.scalar.activation(out=zero[:], in_=zero[:], func=ACT.Square)
            load_zgc("c", 0, 0)
            sq(0, 0)
            load_zgc("g", 0, 0, 0)
            load_zgc("z", 0, 0, 0)
            s1(0, 0, 0)
            load_zgc("z", 0, 0, 1)
            load_zgc("g", 0, 0, 1)
            s1(0, 0, 1)
            s2(0, 0)
            tr(0, 0)
            load_zgc("g", 0, 1)
            load_zgc("c", 0, 1)
            load_zgc("z", 0, 1)
            s1(0, 1)
            sq(0, 1)
            s2(0, 1)
            tr(0, 1)
            load_zgc("z", 1, None)
            load_zgc("g", 1, None)
            load_zgc("c", 1, None)
            load_zgc("g", 2, None)
            load_xs()
            load_x(0)
            load_zgc("z", 2, None)
            load_zgc("c", 2, None)
            load_zgc("z", 3, None)
            load_quad("r", 0)
            load_zgc("g", 3, None)
            load_zgc("c", 3, None)
            load_quad("h", 0)
            load_us(0), load_us(1), load_us(2), load_us(3), load_uw()
            load_quad("h", 1)
            load_quad("r", 1)
            load_x(1)
            tcp(0, 0, S)
            sq(1, 1)
            sq(1, 0)
            tcp(0, 1, S)
            widen(0, 1, S)
            widen(0, 2, S)
            s1(1, 1)
            s1(1, 0)
            s2(1, 1)
            s2(1, 0)
            qe(0)
            s1(2, 0)
            s1(2, 1)
            sq(2, 0)
            s2(2, 0)
            tr(1, 0)
            tr(1, 1)
            tr(2, 0)
            sq(2, 1)
            widen(0, 0, S)
            widen(0, 3, S)
            tcp(1, 0, S)
            tcp(1, 1, S)
            tcp(2, 0, S)
            s2(2, 1)
            t1(0, 0)
            s1(3, 1)
            s1(3, 0)
            qe(1)
            sq(3, 0)
            sq(3, 1)
            tr(2, 1)
            s2(3, 0)
            s2(3, 1)
            tr(3, 0)
            tr(3, 1)
            pe_da(1, 0, 0)
            pe_da(1, 0, 1)
            pe_da(0, 0, 1)
            pe_da(0, 0, 0)
            il_cp("h", 0, 0, S)
            tcp(2, 1, S)
            il_cp("h", 0, 1, S)
            tcp(3, 1, S)
            tcp(3, 0, S)
            t1(0, 1)
            wop(0, 0)
            wop(0, 1)
            qe(3)
            drop(1, 0, 1)
            qe(2)
            drop(1, 0, 0)
            t1(1, 1)
            il_cp("x", 0, 1, S)
            il_cp("h", 1, 0, S)
            il_cp("h", 1, 1, S)
            drop(0, 0, 1)
            pe_da(1, 1, 0)
            pe_da(1, 1, 1)
            wop(1, 1)
            drop(0, 0, 0)
            drop(1, 1, 0)
            drop(1, 1, 1)
            q_w("h", 0)
            qdr(1)
            pe_da(0, 1, 0)
            widen(1, 0, S)
            widen(1, 2, S)
            widen(1, 1, S)
            widen(1, 3, S)
            il_cp("x", 1, 0, S)
            pe_da(0, 1, 1)
            pe_da(2, 0, 0)
            pe_da(2, 1, 1)
            o_mm("h", (0, 1), (1,))
            il_cp("x", 1, 1, S)
            o_cp("h", (0, 1), (1,), (0, 1, 2, 3), (1,), S)
            il_cp("x", 0, 0, S)
            t1(1, 0)
            q_w("h", 1)
            wop(1, 0)
            q_w("x", 1)
            drop(0, 1, 0)
            drop(0, 1, 1)
            q_w("x", 0)
            qdr(0)
            t1(0, 2)
            t1(1, 2)
            o_mm("h", (2, 3), (1,))
            o_mm("x", (2, 3), (1,))
            o_cp("h", (2, 3), (1,), (0, 1, 2, 3), (1,), S)
            pe_da(2, 1, 0)
            o_mm("x", (0, 1), (1,))
            o_mm("h", (0, 1), (0,))
            o_mm("h", (2, 3), (0,))
            il_cp("h", 0, 2, S)
            o_cp("x", (2, 3), (1,), (0, 1, 2, 3), (1,), S)
            il_cp("h", 1, 2, S)
            wop(0, 2)
            o_cp("x", (0, 1), (1,), (0, 1, 2, 3), (1,), S)
            o_cp("h", (0, 1), (0,), (0, 1, 2, 3), (0,), S)
            il_cp("h", 1, 3, S)
            o_cp("h", (2, 3), (0,), (0, 1, 2, 3), (0,), S)
            il_cp("h", 0, 3, S)
            q_w("h", 2)
            drop(2, 0, 0)
            wop(1, 2)
            q_w("h", 3)
            o_mm("x", (2, 3), (0,))
            pe_da(2, 0, 1)
            o_mm("x", (0, 1), (0,))
            o_mm("h", (4, 5), (1,))
            pe_da(3, 1, 0)
            o_mm("h", (4, 5), (0,))
            o_cp("x", (2, 3), (0,), (0, 1, 2, 3), (0,), S)
            o_cp("x", (0, 1), (0,), (0, 1, 2, 3), (0,), S)
            o_cp("h", (4, 5), (1,), (4, 5, 6, 7), (1,), S)
            o_cp("h", (4, 5), (0,), (4, 5, 6, 7), (0,), S)
            drop(2, 0, 1)
            drop(2, 1, 1)
            drop(2, 1, 0)
            qdr(2)
            t1(0, 3)
            t1(1, 3)
            wop(0, 3)
            wop(1, 3)
            o_st("h", (0, 1, 2, 3), (1,))
            o_st("x", (0, 1, 2, 3), (1,))
            o_st("h", (0, 1, 2, 3), (0,))
            o_st("x", (0, 1, 2, 3), (0,))
            o_mm("h", (6, 7), (0,))
            o_mm("h", (6, 7), (1,))
            pe_da(3, 0, 0)
            pe_da(4, 0, 0)
            o_cp("h", (6, 7), (0,), (4, 5, 6, 7), (0,), S)
            o_st("h", (4, 5, 6, 7), (0,))
            o_cp("h", (6, 7), (1,), (4, 5, 6, 7), (1,), S)
            il_cp("x", 0, 2, S)
            o_st("h", (4, 5, 6, 7), (1,))
            o_mm("h", (0, 1), (2,))
            o_cp("h", (0, 1), (2,), (0, 1, 2, 3), (2,), S)
            o_mm("h", (2, 3), (2,))
            o_cp("h", (2, 3), (2,), (0, 1, 2, 3), (2,), S)
            o_st("h", (0, 1, 2, 3), (2,))
            o_mm("h", (4, 5), (2,))
            o_mm("h", (6, 7), (2,))
            o_mm("x", (0, 1), (2,))
            o_mm("x", (2, 3), (2,))
            pe_da(4, 1, 0)
            o_cp("h", (4, 5), (2,), (4, 5, 6, 7), (2,), S)
            o_cp("h", (6, 7), (2,), (4, 5, 6, 7), (2,), S)
            o_cp("x", (0, 1), (2,), (0, 1, 2, 3), (2,), S)
            o_cp("x", (2, 3), (2,), (0, 1, 2, 3), (2,), S)
            o_st("h", (4, 5, 6, 7), (2,))
            il_cp("x", 1, 2, S)
            drop(3, 0, 0)
            drop(3, 1, 0)
            t1(0, 4)
            qdr(3)
            t1(1, 4)
            wop(0, 4)
            wop(1, 4)
            q_w("x", 2)
            drop(4, 1, 0)
            drop(4, 0, 0)
            qdr(4)
            o_mm("x", (0, 1, 2, 3), (3,))
            o_mm("h", (4, 5, 6, 7), (3,))
            o_mm("h", (0, 1, 2, 3), (3,))
            o_st("x", (0, 1, 2, 3), (2,))
            o_cp("x", (0, 1, 2, 3), (3,), (0, 1, 2, 3), (3,), S)
            o_cp("h", (4, 5, 6, 7), (3,), (4, 5, 6, 7), (3,), S)
            o_cp("h", (0, 1, 2, 3), (3,), (0, 1, 2, 3), (3,), S)
            o_mm("x", (4,), (0, 1))
            o_mm("x", (5,), (0, 1))
            o_cp("x", (4,), (0, 1), (4, 5), (0, 1), S)
            o_cp("x", (5,), (0, 1), (4, 5), (0, 1), S)
            o_st("x", (0, 1, 2, 3), (3,))
            o_st("h", (4, 5, 6, 7), (3,))
            o_st("h", (0, 1, 2, 3), (3,))
            o_st("x", (4, 5), (0, 1))
            o_mm("h", (4, 5, 6, 7), (4,))
            o_cp("h", (4, 5, 6, 7), (4,), (4, 5, 6, 7), (4,), S)
            o_mm("h", (0, 1, 2, 3), (4,))
            o_cp("h", (0, 1, 2, 3), (4,), (0, 1, 2, 3), (4,), S)
            o_st("h", (4, 5, 6, 7), (4,))
            o_st("h", (0, 1, 2, 3), (4,))
            o_mm("x", (4,), (2, 3, 4))
            o_mm("x", (5,), (2, 3, 4))
            o_cp("x", (4,), (2, 3, 4), (4, 5), (2, 3, 4), S)
            o_cp("x", (5,), (2, 3, 4), (4, 5), (2, 3, 4), S)
            o_st("x", (4, 5), (2, 3, 4))
            o_mm("x", (0, 1, 2, 3), (4,))
            o_cp("x", (0, 1, 2, 3), (4,), (0, 1, 2, 3), (4,), S)
            o_st("x", (0, 1, 2, 3), (4,))
            il_cp("x", 1, 3, V)
            il_cp("x", 0, 3, V)
            q_w("x", 3)
            o_mm("x", (6,), (0, 1))
            o_mm("x", (7,), (0, 1))
            o_cp("x", (6,), (0, 1), (6, 7), (0, 1), V)
            o_cp("x", (7,), (0, 1), (6, 7), (0, 1), V)
            o_st("x", (6, 7), (0, 1))
            o_mm("x", (6,), (2, 3, 4))
            o_cp("x", (6,), (2, 3, 4), (6, 7), (2, 3, 4), V)
            o_mm("x", (7,), (2, 3, 4))
            o_cp("x", (7,), (2, 3, 4), (6, 7), (2, 3, 4), S)
            o_st("x", (6, 7), (2, 3, 4))
